import numpy as np, ml_dtypes
CORES = [51,54,179,182]
N = 4
BF = ml_dtypes.bfloat16
V, M, C, B, VIS, H, ST = 2048, 256, 1024, 8, 5, 10, 1
def pack(v, words, rel, om, th):
    return {"x": np.ascontiguousarray(v.reshape(N, 128, V)).astype(np.float32).astype(BF), "wd": np.ascontiguousarray(words.reshape(N, 128, M)).astype(np.int32),
            "rt": np.ascontiguousarray(rel.reshape(N, 128, C)).astype(np.int32), "wt": np.ascontiguousarray(om.reshape(N, 128, 1)).astype(np.int32), "th": np.ascontiguousarray(th.reshape(N, 128, 1)).astype(np.int32)}
def setup_inputs(rng):
    return pack(rng.integers(0, 256, (N, 8, 16, V)), rng.integers(0, V, (N, 8, 16, M)), rng.integers(0, V, (N, 8, 16, C)), rng.integers(0, 4096, (N, 8, 16)), rng.integers(1500, 1751, (N, 8, 16)))
def setup_inputs_spread(rng):
    v = np.floor(256 * rng.random((N, 8, 16, V)) * np.exp2(-8 * rng.random((N, 8, 1, V)))).astype(np.int64)
    om = np.floor(4096 * np.exp2(-12.5 * rng.random((N, 8, 16)))).astype(np.int64)
    lev = rng.choice(np.array([300, 700, 1200, 2500, 4080]), (N, 8, 1)); th = np.floor(lev * (0.6 + 0.4 * rng.random((N, 8, 16)))).astype(np.int64)
    pw = rng.choice(np.array([1.0, 1.5, 2.0, 3.0]), (N, 8, 1, 1))
    words = np.floor(V * rng.random((N, 8, 16, M)) ** pw).astype(np.int64); rel = np.floor(V * rng.random((N, 8, 16, C)) ** pw).astype(np.int64)
    return pack(np.minimum(v, 255), np.minimum(words, V - 1), np.minimum(rel, V - 1), np.minimum(om, 4095), np.minimum(th, 4080))
def setup_inputs_ends(rng):
    v = 255 * rng.integers(0, 2, (N, 8, 16, V)); full = rng.random((N, 8)) < 0.5; full[:, 6:] = True
    v[full, :, V - 16:] = 255; v[full, :, 0] = 0
    om = 4095 * rng.integers(0, 2, (N, 8, 16))
    for q in range(N):
        a = 7 - (N - 1 - q) % 2; om[q, 6:] = 4095; om[q, 13 - a, 15] = 272
    hit = [((u * u >> 5) + 37 * u) & (C - 1) for u in (0, 16, 4095)]
    words = (V - 1) * rng.integers(0, 2, (N, 8, 16, M)); mix = rng.random((N, 8, 1, M)) < 0.2; mix[..., 0] = False; mix[..., M - 1] = False
    words = np.where(mix, rng.integers(0, V, (N, 8, 16, M)), words); words[:, :, 0, M - 1] = V - 1; words[:, :, 0, 0] = 0
    rel = (V - 1) * rng.integers(0, 2, (N, 8, 16, C)); mix = rng.random((N, 8, 1, C)) < 0.2; mix[..., hit] = False
    rel = np.where(mix, rng.integers(0, V, (N, 8, 16, C)), rel)
    rel[:, 6:, :, 0] = V - 16 + np.arange(16)
    for c in hit[1:]:
        rel[:, 6:, :, c] = 0; rel[:, 6:, 6, c] = V - 1; rel[:, 6:, 15, c] = V - 1
    pre = rng.choice(np.array([0, 4, H - 1, H, 12, 16]), (N, 8)); pre[:, 0] = 0; pre[:, 6] = 12; pre[:, 7] = 16
    th = 4080 * (np.arange(16) < pre[:, :, None]).astype(np.int64)
    for q in range(N):
        if (N - 1 - q) % 2 == 1:
            th[q, 7, 15] = 4079; th[q, 6, H - 1] = 4079
        else:
            th[q, 6, 11] = 4079
    return pack(v, words, rel, om, th)
def setup_inputs_corners(rng):
    val = np.array([0, 8, 9, 247, 248, 249]); cls = rng.choice(6, (N, 8, V), p=[0.4, 0.1, 0.1, 0.1, 0.2, 0.1])
    cls[:, ::2, 0] = 0; cls[:, 1::2, 0] = 4; cls[:, ::2, V - 1] = 4; cls[:, 1::2, V - 1] = 0
    ft = rng.integers(0, 16, (N, 8, 1, V)); v = rng.integers(0, 7, (N, 8, 16, 1)) + np.where(np.arange(16).reshape(16, 1) == ft, val[cls][:, :, None, :], 0)
    cnt = np.array([31, 8 * M, 33, 0, 63, 32, 1, 64]); order = rng.permutation(N); kk = np.arange(16).reshape(16, 1)
    words = np.zeros((N, 8, 16, M), np.int64); rel = np.zeros((N, 8, 16, C), np.int64); om = np.zeros((N, 8, 16), np.int64)
    for q in range(N):
        hit = (rng.permutation(8 * M) < int(cnt[order[q]])).reshape(8, M)
        lw = np.where(hit, rng.choice(np.array([H, 12, 15, 16]), (8, M)), rng.choice(np.array([0, 1, H - 1]), (8, M)))
        for g in range(8):
            z = np.flatnonzero(cls[q, g] == 0); b = np.flatnonzero(cls[q, g] != 0)
            za = z[rng.integers(0, len(z), (16, M))]; bb = b[rng.integers(0, len(b), (16, M))]
            words[q, g] = np.where(kk < lw[g], za, np.where(kk == lw[g], bb, rng.integers(0, V, (16, M))))
            rel[q, g] = z[rng.integers(0, len(z), (16, C))]
            m = (q + g) % 4
            if m == 1: om[q, g, int(rng.integers(0, 16))] = 4095
            if m == 2: om[q, g] = 4095
            if m == 3: om[q, g] = rng.integers(0, 4096, 16)
    return pack(v, words, rel, om, rng.choice(np.array([0, 0, 1]), (N, 8, 16)))
def setup_inputs_ties(rng):
    pr = rng.integers(0, 256, (N, 8, 16, 6)); v = np.take_along_axis(pr, rng.integers(0, 6, (N, 8, 1, V)), 3)
    dd = np.sort(np.add.reduce(np.abs(pr[:, :, :, :, None] - pr[:, :, :, None, :]), axis=2).reshape(N, 8, 36), axis=2)
    ix = np.minimum(rng.choice(np.array([20, 28, 33]), (N, 8, 1)) + rng.integers(0, 8, (N, 8, 16)), 35)
    th = np.maximum(np.take_along_axis(dd, ix, 2) - rng.integers(0, 2, (N, 8, 16)), 0)
    words = rng.integers(0, V, (N, 8, 16, M)); words[:, :, :, ::3] = words[:, :, :1, ::3].copy()
    rel = rng.integers(0, V, (N, 8, 16, C)); rel[:, :, :, ::4] = rel[:, :, :1, ::4].copy()
    om = rng.integers(0, 4096, (N, 8, 16))
    for q in range(N):
        for g in range(1, 8, 2):
            b = int(rng.integers(1, V - 2)); a = rng.integers(0, 100, 16)
            v[q, g, :, b] = a; v[q, g, :, b + 1] = a + 150; v[q, g, :, V - 1] = a + 100; v[q, g, :, 0] = a + 100; v[q, g, int(rng.integers(0, 16)), 0] += 1
            u = int(np.add.reduce(om[q, g] * a)) & 4095; c = ((u * u >> 5) + 37 * u) & (C - 1)
            rel[q, g, :, c] = b + 1; rel[q, g, 0, c] = 0; rel[q, g, 15, c] = V - 1
            words[q, g, 0, 1::8] = b; th[q, g, 0] = 1600
    return pack(v, words, rel, om, th)
def setup_inputs_still(rng):
    far = V // 2 + rng.permutation(V // 2)[:V // 4]; zero = rng.permutation(np.setdiff1d(np.arange(V), far))[:V // 4]
    val = rng.choice(np.array([1, 8, 9, 100, 248]), (N, 8, V)); val[..., zero] = 0; val[..., far] = 0
    ft = rng.integers(0, 16, (N, 8, 1, V)); kk = np.arange(16).reshape(16, 1)
    v = rng.integers(0, 7, (N, 8, 16, 1)) + np.where(kk == ft, val[:, :, None, :], 0)
    v[:, :, 2:5, far] = 255 - rng.integers(0, 7, (N, 8, 3, V // 4))
    words = np.where((kk + rng.integers(0, 4, (N, 8, 1, M))) % 4 == 0, far[rng.integers(0, V // 4, (N, 8, 16, M))], rng.integers(0, V, (N, 8, 16, M)))
    rel = zero[rng.integers(0, V // 4, (N, 8, 16, C))]
    cnt = rng.permutation(np.array([1, 31, 33, 63])); par = int(rng.integers(0, 2))
    for q in range(par, N, 2):
        hit = np.zeros((8, M), bool); hit[:, :M // 2] = (rng.permutation(8 * (M // 2)) < int(cnt[q // 2])).reshape(8, M // 2)
        lw = rng.choice(np.array([H, 12, 16]), (8, 1, M))
        w = np.where(kk < lw, zero[rng.integers(0, V // 4, (8, 16, M))], far[rng.integers(0, V // 4, (8, 16, M))])
        words[q] = np.where(hit[:, None, :], w, words[q])
    return pack(v, words, rel, rng.integers(0, 4096, (N, 8, 16)), rng.choice(np.array([0, 0, 1]), (N, 8, 16)))
def check_inputs(d):
    bad = []
    for k, hi in (("x", 255), ("wd", V - 1), ("rt", V - 1), ("wt", 4095), ("th", 4080)):
        v = np.asarray(d[k]).astype(np.float64)
        if not (np.min(v) >= 0 and np.max(v) <= hi): bad.append("range of " + k)
        elif np.any(v != np.floor(v)): bad.append("whole numbers of " + k)
    return bad
def reference(x, wd, rt, wt, th):
    X = x.astype(np.float32).astype(np.int32).reshape(N, 8, 16, V)
    W = wd.astype(np.int64).reshape(N, 8, 16, M); RT = rt.astype(np.int64).reshape(N, 8, 16, C)
    om = wt.astype(np.int64).reshape(N, 8, 16, 1); lim = th.astype(np.int64).reshape(N, 8, 16, 1)
    A = np.zeros(N, np.int64); k = np.arange(16).reshape(1, 1, 16, 1); i = np.arange(M).reshape(1, 1, M)
    def pick(c):
        return np.take_along_axis(X, c.reshape(N, 8, 1, 16 * M), 3).reshape(N, 8, 16, 16, M)
    for t in range(VIS):
        if t > 0:
            W = np.roll(np.roll(W, ST, axis=0), (t + t // N) - (t - 1 + (t - 1) // N), axis=1)
        xw = pick(W); x0 = xw[:, :, :, 0]
        u = np.add.reduce(om * x0, axis=2) & 4095
        c = ((u * u >> 5) + 37 * u) & (C - 1)
        R = np.take_along_axis(RT, c[:, :, None, :], 3)
        s = np.argmin(np.add.reduce(np.abs(pick(R) - x0[:, :, :, None, :]), axis=2), axis=2)
        Q = np.take_along_axis(R, (s[:, :, None, :] + k) & 15, 2)
        xq = pick(Q); gap = np.add.reduce(np.abs(xw - xq), axis=2)
        ok = (gap <= lim + 8 * (A & 31).reshape(N, 1, 1, 1)).astype(np.int64)
        l = np.add.reduce(np.minimum.accumulate(ok, axis=2), axis=2)[:, :, None, :]
        rep = l >= H; uu = u[:, :, None, :]
        new = np.where(k < 16 - l, Q[:, :, ::-1] ^ 1, np.where(k < 32 - 2 * l, np.take_along_axis(W, (k + 2 * l - 16) & 15, 2), ((Q * uu >> 5) + Q) & (V - 1)))
        W = np.where(rep, new, np.take_along_axis(W, (k + l + 1) & 15, 2))
        at = (B * i + (u & (B - 1)))[:, :, None, :]
        np.put_along_axis(X, at, np.where(rep, (x0 + xq[:, :, :, 15]) >> 1, np.take_along_axis(X, at, 3)), 3)
        A = np.add.reduce(rep.reshape(N, 8 * M).astype(np.int64), axis=1)
    return {"yx": X.reshape(N, 128, V).astype(np.float32).astype(BF), "yw": W.reshape(N, 128, M).astype(np.float32)}

@@ -1,0 +1,605 @@
+from concourse.bass import DstId, RemoteDMATransfer
+from concourse.mybir import dt, AluOpType, AxisListType, ActivationFunctionType
+
+ALU = AluOpType
+ACT = ActivationFunctionType
+NV = 5
+NRT = 1
+NM = 35
+MQ, MW, MH, REV = 16, 22, 28, 34
+V = 2048
+
+SCRATCH = {
+    "xv": ("sbuf", [128, 2304], "bfloat16"),
+    "wdi": ("sbuf", [128, 256], "int32"), "rti": ("sbuf", [128, 1024], "int32"),
+    "wti": ("sbuf", [128, 8], "int32"), "thi": ("sbuf", [128, 8], "int32"),
+    "wd16": ("sbuf", [128, 256], "float16"), "rt16": ("sbuf", [128, 1024], "float16"),
+    "RT0": ("sbuf", [128, 1024], "float32"),
+    "RTR": ("sbuf", [128, 16384], "float32"), "RD": ("dram", [8, 32, 1024], "float32"),
+    "RTab": ("sbuf", [128, 4096], "float32"), "NT": ("sbuf", [128, 2 * 17 * 128], "float32"),
+    "W0": ("sbuf", [128, 256], "uint16"), "W1": ("sbuf", [128, 256], "uint16"), "W2": ("sbuf", [128, 256], "uint16"),
+    "W3": ("sbuf", [128, 256], "uint16"), "W4": ("sbuf", [128, 256], "uint16"),
+    "S0": ("sbuf", [128, 256], "uint16"), "S1": ("sbuf", [128, 256], "uint16"), "S2": ("sbuf", [128, 256], "uint16"),
+    "S3": ("sbuf", [128, 256], "uint16"),
+    "w16": ("sbuf", [128, 256], "float16"),
+    "xw": ("sbuf", [128, 4096], "bfloat16"), "Z": ("sbuf", [128, 4096], "bfloat16"), "X0": ("sbuf", [128, 4096], "bfloat16"),
+    "d": ("sbuf", [128, 4096], "bfloat16"), "ad": ("sbuf", [128, 16, 256], "bfloat16"),
+    "hold": ("sbuf", [128, 2048], "bfloat16"),
+    "row": ("sbuf", [128, 144], "int32"), "grow": ("sbuf", [128, 128], "int32"), "krow": ("sbuf", [128, 128], "int32"),
+    "pc": ("sbuf", [128, 8], "int32"), "ai": ("sbuf", [128, 16], "int32"), "gam": ("sbuf", [128, 16], "int32"),
+    "ki": ("sbuf", [128, 8], "int32"), "gi": ("sbuf", [128, 8], "int32"),
+    "pf": ("sbuf", [128, 8], "float32"), "kf": ("sbuf", [128, 8], "float32"), "gf": ("sbuf", [128, 8], "float32"),
+    "g16": ("sbuf", [128, 8], "float32"), "whi_i": ("sbuf", [128, 8], "int32"), "wlo_i": ("sbuf", [128, 8], "int32"),
+    "whi": ("sbuf", [128, 8], "float32"), "wlo": ("sbuf", [128, 8], "float32"), "thf": ("sbuf", [128, 8], "float32"),
+    "kr15": ("sbuf", [128, 8], "float32"), "bm": ("sbuf", [128, 16], "float32"),
+    "tgt": ("sbuf", [128, 560], "int32"), "tga": ("sbuf", [128, 256], "int32"),
+    "F1": ("sbuf", [128, 35, 16], "bfloat16"), "CM": ("sbuf", [128, 35, 160], "bfloat16"),
+    "EZ": ("sbuf", [128, 144], "bfloat16"), "ED": ("sbuf", [128, 144], "bfloat16"),
+    "WZh": ("sbuf", [128, 144], "bfloat16"), "WZl": ("sbuf", [128, 144], "bfloat16"),
+    "WBh": ("sbuf", [128, 128], "bfloat16"), "WBl": ("sbuf", [128, 128], "bfloat16"),
+    "BO": ("sbuf", [128, 128], "float32"), "thr": ("sbuf", [128, 128], "float32"),
+    "IB": ("sbuf", [128, 128], "bfloat16"), "I4": ("sbuf", [128, 128], "bfloat16"), "IM": ("sbuf", [128, 128], "bfloat16"),
+    "rot": ("sbuf", [128, 3, 128], "float32"),
+    "ones": ("sbuf", [128, 128], "bfloat16"), "jrow": ("sbuf", [128, 64], "bfloat16"), "rs": ("sbuf", [128, 128], "float32"),
+    "okb": ("sbuf", [128, 256], "bfloat16"), "hs": ("sbuf", [128, 256], "bfloat16"), "ilc": ("sbuf", [128, 16], "float32"),
+    "fm": ("sbuf", [128, 16], "float32"), "yb": ("sbuf", [128, 16], "float32"),
+    "ilf": ("sbuf", [128, 16], "float32"), "ili": ("sbuf", [128, 16], "int32"), "i8": ("sbuf", [128, 16], "float32"),
+    "dm": ("sbuf", [128, 16], "float32"), "TH": ("sbuf", [128, 128], "float32"), "THe": ("sbuf", [128, 128], "float32"),
+    "ui": ("sbuf", [128, 16], "int32"), "uu": ("sbuf", [128, 16], "int32"), "tf": ("sbuf", [128, 16], "float32"),
+    "zz": ("sbuf", [128, 16], "int32"), "cc": ("sbuf", [128, 16], "int32"), "cl": ("sbuf", [128, 16], "uint16"),
+    "u7": ("sbuf", [128, 16], "int32"), "at": ("sbuf", [128, 16], "float32"), "km": ("sbuf", [128, 256], "float32"),
+    "kk": ("sbuf", [128, 16], "int32"), "ks": ("sbuf", [128, 16], "int32"), "kq": ("sbuf", [128, 16], "int32"),
+    "qo": ("sbuf", [128, 16], "uint16"), "rl": ("sbuf", [128, 256], "uint16"), "ql": ("sbuf", [128, 256], "uint16"),
+    "r16": ("sbuf", [128, 256], "float16"),
+    "q16": ("sbuf", [128, 256], "float16"), "n16": ("sbuf", [128, 256], "float16"), "qc": ("sbuf", [128, 256], "float16"),
+    "uli": ("sbuf", [128, 256], "int32"), "ulm": ("sbuf", [128, 256], "int32"), "ul": ("sbuf", [128, 256], "float32"),
+    "zi": ("sbuf", [128, 256], "int32"), "hi": ("sbuf", [128, 256], "int32"), "h16": ("sbuf", [128, 256], "float16"),
+    "fo": ("sbuf", [128, 16], "float32"), "fl": ("sbuf", [128, 16], "uint16"), "rp": ("sbuf", [128, 16], "bfloat16"),
+    "s1": ("sbuf", [128, 16], "float32"), "s2": ("sbuf", [128, 16], "float32"), "sl": ("sbuf", [128, 16], "uint16"),
+    "nv": ("sbuf", [128, 256], "int32"), "aj": ("sbuf", [128, 16], "float32"), "ac": ("sbuf", [128, 8], "float32"),
+    "aci": ("sbuf", [128, 8], "int32"), "acm": ("sbuf", [128, 8], "int32"), "a8": ("sbuf", [128, 8], "float32"),
+    "yf": ("sbuf", [128, 256], "float16"), "yo": ("sbuf", [128, 256], "float32"),
+    "P0": ("psum", [128, 512], "float32"), "P1": ("psum", [128, 512], "float32"),
+    "L0": ("psum", [128, 512], "float32"), "L1": ("psum", [128, 512], "float32"),
+    "E0": ("psum", [128, 512], "float32"), "E1": ("psum", [128, 512], "float32"),
+    "E2": ("psum", [128, 512], "float32"), "E3": ("psum", [128, 512], "float32"),
+}
+PSUM = ("P0", "P1", "L0", "L1", "E0", "E1", "E2", "E3")
+SEMAPHORES = (["qv", "qs", "qt", "qg", "ls"] + ["ld%d" % k for k in range(8)] + ["rd", "rtl", "out0", "out1"]
+              + ["ar%d_%d" % (t, h) for t in range(1, NV) for h in range(2)])
+GSH = [(t + t // 4) - (t - 1 + (t - 1) // 4) for t in range(1, NV)] + [0]
+
+
+def rank_program(g, core, T, topo):
+    rank = T.rank_of(core)
+    if rank is None:
+        return
+    n = len(T.cores)
+    nxt, prv = T.cores[(rank + 1) % n], T.cores[(rank - 1) % n]
+
+    Q = {"v": g.vector, "s": g.scalar, "t": g.tensor, "g": g, "y": g.sync}
+    cnt = {"v": 0, "s": 0, "t": 0, "g": 0}
+    seen = {q: {} for q in Q}
+    snap = {}
+    acc = {}
+
+    def need(q, tok):
+        s, val = tok
+        if seen[q].get(s, 0) >= val:
+            return
+        Q[q].wait_ge(T.sem[s], val)
+        seen[q][s] = val
+        for s2, v2 in snap.get(tok, {}).items():
+            if seen[q].get(s2, 0) < v2:
+                seen[q][s2] = v2
+
+    def deps(q, reads, writes):
+        toks = {}
+        for (regs, wr) in ((reads, False), (writes, True)):
+            for (b, lo, hi) in regs:
+                for (l2, h2, q2, tok, w2) in acc.get(b, []):
+                    if b in PSUM:
+                        if q2 == q:
+                            continue
+                    else:
+                        if l2 >= hi or h2 <= lo or not (wr or w2):
+                            continue
+                        if q2 == q and (wr or not w2):
+                            continue
+                    toks[tok[0]] = max(toks.get(tok[0], 0), tok[1])
+        for s in sorted(toks):
+            need(q, (s, toks[s]))
+
+    def note(q, reads, writes, tok):
+        snap[tok] = dict(seen[q])
+        for (b, lo, hi) in writes:
+            old = acc.get(b, [])
+            if b in PSUM:
+                acc[b] = [e for e in old if e[2] != q and e[4] and False] + [[lo, hi, q, tok, True]]
+            else:
+                acc[b] = [e for e in old if not (e[0] >= lo and e[1] <= hi)] + [[lo, hi, q, tok, True]]
+        for (b, lo, hi) in reads:
+            if b in PSUM:
+                acc[b] = [[lo, hi, q, tok, True]]
+            else:
+                acc[b] = [e for e in acc.get(b, []) if not (e[2] == q and not e[4] and e[0] >= lo and e[1] <= hi)] + [[lo, hi, q, tok, False]]
+
+    def op(q, fn, reads, writes):
+        deps(q, reads, writes)
+        cnt[q] += 1
+        s = "q" + q
+        fn().then_inc(T.sem[s], 1)
+        note(q, reads, writes, (s, cnt[q]))
+
+    def dma(q, out, in_, reads, writes, sem, total):
+        deps(q, reads, writes)
+        Q[q].dma_start(out, in_).then_inc(T.sem[sem], 16)
+        note("dma_" + sem, reads, writes, (sem, total)) if False else None
+        snap[(sem, total)] = dict(seen[q])
+        for (b, lo, hi) in writes:
+            acc.setdefault(b, []).append([lo, hi, "dma", (sem, total), True])
+        for (b, lo, hi) in reads:
+            acc.setdefault(b, []).append([lo, hi, "dma", (sem, total), False])
+
+    A_ = lambda b, lo=0, hi=1 << 20: (b, lo, hi)
+    vec, sca, ten = g.vector, g.scalar, g.tensor
+
+    def tcopy(out, in_, r, w):
+        op("v", lambda: vec.tensor_copy(out, in_), r, w)
+
+    def tt(out, a, b, o, r, w):
+        op("v", lambda: vec.tensor_tensor(out, a, b, o), r, w)
+
+    def ts(out, a, s1, s2, o0, o1, r, w):
+        if o1 is None:
+            op("v", lambda: vec.tensor_scalar(out, a, s1, None, o0), r, w)
+        else:
+            op("v", lambda: vec.tensor_scalar(out, a, s1, s2, o0, o1), r, w)
+
+    def mset(ap, c, w):
+        op("v", lambda: vec.memset(ap, c), [], w)
+
+    def actv(out, in_, f, r, w, **kw):
+        op("s", lambda: sca.activation(out, in_, f, **kw), r, w)
+
+    def mm(out, l, r_, st, sp, r, w):
+        op("t", lambda: ten.matmul(out, l, r_, st, sp), r, w)
+
+    def iota(out, pat, base, cm, w):
+        op("g", lambda: g.iota(out, pat, base, cm), [], w)
+
+    dma("s", T.wdi[:], T.wd[:], [], [A_("wdi")], "ld0", 16)
+    dma("y", T.xv[:, 0:V], T.x[:], [], [A_("xv")], "ld1", 16)
+    dma("s", T.rti[:, 712:1024], T.rt[:, 0:312], [], [A_("rti", 712, 1024)], "ld2", 16)
+    dma("s", T.rti[:, 0:712], T.rt[:, 312:1024], [], [A_("rti", 0, 712)], "ld3", 16)
+    dma("y", T.wti[:, 0:1], T.wt[:], [], [A_("wti")], "ld4", 16)
+    dma("y", T.thi[:, 0:1], T.th[:], [], [A_("thi")], "ld5", 16)
+
+    iota(T.pc[:, 0:1], [[1, 1]], 0, 1, [A_("pc")])
+    iota(T.row[:, 0:144], [[1, 144]], 0, 0, [A_("row")])
+    iota(T.grow[:], [[1, 8], [0, 16]], 0, 0, [A_("grow")])
+    iota(T.krow[:], [[0, 8], [1, 16]], 0, 0, [A_("krow")])
+    iota(T.gam[:, 0:10], [[1, 10]], 6, 0, [A_("gam")])
+    iota(T.ai[:], [[16, 16]], 0, 0, [A_("ai")])
+    iota(T.tga[:], [[-1, 16], [1, 16]], 16, 0, [A_("tga")])
+    mset(T.tgt[:, 256:560], -1, [A_("tgt", 256, 560)])
+    iota(T.tgt[:, REV * 16:REV * 16 + 16], [[-1, 16]], 15, 0, [A_("tgt", REV * 16, REV * 16 + 16)])
+    for l in range(10, 16):
+        a = (MQ + l - 10) * 16
+        iota(T.tgt[:, a + l:a + 16], [[-1, 16 - l]], 15 - l, 0, [A_("tgt", a + l, a + 16)])
+        a = (MW + l - 10) * 16
+        iota(T.tgt[:, a + 2 * l - 16:a + l], [[1, 16 - l]], 0, 0, [A_("tgt", a + 2 * l - 16, a + l)])
+        a = (MH + l - 10) * 16
+        iota(T.tgt[:, a:a + 2 * l - 16], [[1, 2 * l - 16]], 0, 0, [A_("tgt", a, a + 2 * l - 16)])
+
+    ts(T.ki[:, 0:1], T.pc[:, 0:1], 15, None, ALU.bitwise_and, None, [A_("pc")], [A_("ki")])
+    ts(T.gi[:, 0:1], T.pc[:, 0:1], 4, None, ALU.logical_shift_right, None, [A_("pc")], [A_("gi")])
+    tcopy(T.pf[:, 0:1], T.pc[:, 0:1], [A_("pc")], [A_("pf")])
+    tcopy(T.kf[:, 0:1], T.ki[:, 0:1], [A_("ki")], [A_("kf")])
+    tcopy(T.gf[:, 0:1], T.gi[:, 0:1], [A_("gi")], [A_("gf")])
+    ts(T.g16[:, 0:1], T.gf[:, 0:1], 16.0, 15.0, ALU.mult, ALU.add, [A_("gf")], [A_("g16")])
+    ts(T.kr15[:, 0:1], T.kf[:, 0:1], -1.0, 15.0, ALU.mult, ALU.add, [A_("kf")], [A_("kr15")])
+    ts(T.tgt[:, 0:256], T.tga[:], 15, None, ALU.bitwise_and, None, [A_("tga")], [A_("tgt", 0, 256)])
+    ts(T.gam[:, 0:10], T.gam[:, 0:10], 7, None, ALU.bitwise_and, None, [A_("gam")], [A_("gam")])
+    ts(T.bm[:, 0:10], T.gam[:, 0:10], T.gf[:, 0:1], None, ALU.is_equal, None, [A_("gam"), A_("gf")], [A_("bm")])
+    for m in range(NM):
+        pass
+    op("v", lambda: vec.tensor_scalar(T.F1[:], T.tgt[:], T.kf[:, 0:1], None, ALU.is_equal),
+       [A_("tgt"), A_("kf")], [A_("F1")])
+    for j in range(10):
+        o = T.CM[:, :, 16 * j:16 * j + 16]
+        sc = T.bm[:, j:j + 1]
+        if j % 2 == 0:
+            ts(o, T.F1[:], sc, None, ALU.mult, None, [A_("F1"), A_("bm")], [A_("CM", j, j + 1)])
+        else:
+            actv(o, T.F1[:], ACT.Copy, [A_("F1"), A_("bm")], [A_("CM", j, j + 1)], scale=sc)
+
+    def cmat(m, rho):
+        lo = 16 * (2 - rho)
+        return T.CM[:, m, lo:lo + 128], A_("CM", 2 - rho, 10 - rho)
+
+    tcopy(T.wd16[:], T.wdi[:], [A_("wdi")], [A_("wd16")])
+    c, rc = cmat(REV, 0)
+    mm(T.E0[:, 0:256], c, T.wd16[:], True, True, [rc, A_("wd16")], [A_("E0")])
+    tcopy(T.W0[:], T.E0[:, 0:256], [A_("E0")], [A_("W0")])
+    tcopy(T.rt16[:], T.rti[:], [A_("rti")], [A_("rt16")])
+    for k in range(2):
+        e = "E%d" % (1 + k)
+        mm(T[e][:], c, T.rt16[:, 512 * k:512 * k + 512], True, True, [rc, A_("rt16")], [A_(e)])
+        actv(T.RT0[:, 512 * k:512 * k + 512], T[e][:], ACT.Copy, [A_(e)], [A_("RT0", 512 * k, 512 * k + 512)])
+    dma("y", T.RD[:, 0:16, :], T.RT0[:], [A_("RT0")], [A_("RD")], "rd", 32)
+    dma("y", T.RD[:, 16:32, :], T.RT0[:], [A_("RT0")], [], "rd", 32)
+    for s in range(16):
+        dma("y", T.RTR[:, 1024 * s:1024 * s + 1024], T.RD[:, 16 - s:32 - s, :], [A_("RD")], [A_("RTR")] if s == 0 else [], "rtl", 256)
+
+    ts(T.wlo_i[:, 0:1], T.wti[:, 0:1], 255, None, ALU.bitwise_and, None, [A_("wti")], [A_("wlo_i")])
+    ts(T.whi_i[:, 0:1], T.wti[:, 0:1], 3840, None, ALU.bitwise_and, None, [A_("wti")], [A_("whi_i")])
+    tcopy(T.wlo[:, 0:1], T.wlo_i[:, 0:1], [A_("wlo_i")], [A_("wlo")])
+    tcopy(T.whi[:, 0:1], T.whi_i[:, 0:1], [A_("whi_i")], [A_("whi")])
+    sel = [A_("row"), A_("g16")]
+    ts(T.WZh[:], T.row[:], T.g16[:, 0:1], T.whi[:, 0:1], ALU.is_equal, ALU.mult, sel + [A_("whi")], [A_("WZh")])
+    ts(T.WZl[:], T.row[:], T.g16[:, 0:1], T.wlo[:, 0:1], ALU.is_equal, ALU.mult, sel + [A_("wlo")], [A_("WZl")])
+    ts(T.ED[:], T.row[:], T.g16[:, 0:1], 16384.0, ALU.is_equal, ALU.mult, sel, [A_("ED")])
+    ts(T.EZ[:], T.row[:], T.g16[:, 0:1], None, ALU.is_equal, None, sel, [A_("EZ")])
+    ts(T.WBh[:], T.grow[:], T.gf[:, 0:1], T.whi[:, 0:1], ALU.is_equal, ALU.mult, [A_("grow"), A_("gf"), A_("whi")], [A_("WBh")])
+    ts(T.WBl[:], T.grow[:], T.gf[:, 0:1], T.wlo[:, 0:1], ALU.is_equal, ALU.mult, [A_("grow"), A_("gf"), A_("wlo")], [A_("WBl")])
+    mset(T.Z[:], 0.0, [A_("Z")])
+    mset(T.hold[:], 1.0, [A_("hold")])
+    op("v", lambda: vec.memset(T.hold[:, 0:2048:16], 0.0), [A_("hold")], [A_("hold")])
+    mset(T.ones[:], 1.0, [A_("ones")])
+    ts(T.jrow[:], T.krow[:, 0:64], -1024.0, 15360.0, ALU.mult, ALU.add, [A_("krow")], [A_("jrow")])
+    ts(T.rs[:], T.krow[:], 0.0, 1e9, ALU.is_equal, ALU.mult, [A_("krow")], [A_("rs")])
+    ts(T.ilf[:], T.ai[:], T.kf[:, 0:1], None, ALU.add, None, [A_("ai"), A_("kf")], [A_("ilf")])
+    tcopy(T.ili[:], T.ilf[:], [A_("ilf")], [A_("ili")])
+    ts(T.i8[:], T.ilf[:], 8.0, None, ALU.mult, None, [A_("ilf")], [A_("i8")])
+    ts(T.dm[:], T.ilf[:], 2048.0, None, ALU.add, None, [A_("ilf")], [A_("dm")])
+    irow = T.row[:, 0:128]
+    ts(T.IB[:], irow, T.pf[:, 0:1], None, ALU.is_equal, None, [A_("row"), A_("pf")], [A_("IB")])
+
+    def late_constants():
+        ts(T.ilc[:, 0:8], T.ilf[:, 0:8], -128.0, None, ALU.add, None, [A_("ilf")], [A_("ilc")])
+        ts(T.I4[:], irow, T.pf[:, 0:1], 4.0, ALU.is_equal, ALU.mult, [A_("row"), A_("pf")], [A_("I4")])
+        ts(T.IM[:], irow, T.pf[:, 0:1], -1.0, ALU.is_equal, ALU.mult, [A_("row"), A_("pf")], [A_("IM")])
+        tcopy(T.thf[:, 0:1], T.thi[:, 0:1], [A_("thi")], [A_("thf")])
+        ts(T.BO[:], T.grow[:], T.gf[:, 0:1], None, ALU.is_equal, None, [A_("grow"), A_("gf")], [A_("BO")])
+        ts(T.thr[:], T.krow[:], T.kr15[:, 0:1], T.thf[:, 0:1], ALU.is_equal, ALU.mult, [A_("krow"), A_("kr15"), A_("thf")], [A_("thr")])
+        mm(T.L1[:, 384:512], T.BO[:], T.thr[:], True, True, [A_("BO"), A_("thr")], [A_("L1")])
+        tcopy(T.TH[:], T.L1[:, 384:512], [A_("L1")], [A_("TH")])
+        for r in (1, 2):
+            src = T.CM[:, 0, 16 * (2 - r):16 * (2 - r) + 128]
+            tcopy(T.rot[:, r, :], src, [A_("CM")], [A_("rot", r, r + 1)])
+
+    ebank = [0]
+
+    def nextbank():
+        ebank[0] = (ebank[0] + 1) % 4
+        return "E%d" % ebank[0]
+
+    def gather_values(q, t, lo, hi):
+        w = "W%d" % t
+        src = T.xv[:, 0:V].indirect(T[w][:, lo:hi])
+        out = T.xw[:, 16 * lo:16 * hi]
+        r = [A_("xv"), A_(w, lo, hi)]
+        if q == "v":
+            tcopy(out, src, r, [A_("xw", 16 * lo, 16 * hi)])
+        else:
+            actv(out, src, ACT.Copy, r, [A_("xw", 16 * lo, 16 * hi)])
+
+    def pe_u(h):
+        P, L, lo = "P%d" % h, "L%d" % h, 2048 * h
+        rx = A_("xw", lo, lo + 2048)
+        for b in range(16):
+            rhs = T.xw[:, lo + 16 * b + 15:lo + 2048:256]
+            mm(T[P][:, 0:8], T.WZh[:, 15 - b:143 - b], rhs, b == 0, False, [rx, A_("WZh")], [A_(P)])
+            mm(T[P][:, 0:8], T.WZl[:, 15 - b:143 - b], rhs, False, b == 15, [rx, A_("WZl")], [A_(P)])
+        rhs = T.xw[:, lo + 15:lo + 2048:16]
+        mm(T[L][:, 0:128], T.WBh[:], rhs, True, False, [rx, A_("WBh")], [A_(L)])
+        mm(T[L][:, 0:128], T.WBl[:], rhs, False, True, [rx, A_("WBl")], [A_(L)])
+
+    def expand(h):
+        lo = 2048 * h
+        R = lambda b: A_(b, lo, lo + 2048)
+        tcopy(T.Z[:, lo:lo + 2048:16], T.xw[:, lo + 15:lo + 2048:16], [R("xw")], [R("Z")])
+        op("v", lambda: vec.tensor_tensor_scan(T.X0[:, lo:lo + 2048], T.hold[:], T.Z[:, lo:lo + 2048], 0.0, ALU.mult, ALU.add),
+           [A_("hold"), R("Z")], [R("X0")])
+
+    def relators(t, h):
+        P = "P%d" % h
+        c8 = slice(8 * h, 8 * h + 8)
+        R = lambda b: A_(b, 8 * h, 8 * h + 8)
+        tcopy(T.ui[:, c8], T[P][:, 0:8], [A_(P)], [R("ui")])
+        ts(T.uu[:, c8], T.ui[:, c8], 4095, None, ALU.bitwise_and, None, [R("ui")], [R("uu")])
+        ts(T.tf[:, c8], T.uu[:, c8], 592.0, None, ALU.add, None, [R("uu")], [R("tf")])
+        tt(T.zz[:, c8], T.tf[:, c8], T.tf[:, c8], ALU.mult, [R("tf")], [R("zz")])
+        ts(T.cc[:, c8], T.zz[:, c8], 5, 1023, ALU.logical_shift_right, ALU.bitwise_and, [R("zz")], [R("cc")])
+        tcopy(T.cl[:, c8], T.cc[:, c8], [R("cc")], [R("cl")])
+        w = slice(128 * h, 128 * h + 128)
+        RW = lambda b: A_(b, 128 * h, 128 * h + 128)
+        tcopy(T.rl[:, w], T.RT0[:].indirect(T.cl[:, c8]), [A_("RT0"), R("cl")], [RW("rl")])
+        if t < NRT:
+            tcopy(T.r16[:, w], T.rl[:, w], [RW("rl")], [RW("r16")])
+
+    def at_list(h):
+        c8 = slice(8 * h, 8 * h + 8)
+        R = lambda b: A_(b, 8 * h, 8 * h + 8)
+        ts(T.u7[:, c8], T.ui[:, c8], 7, None, ALU.bitwise_and, None, [R("ui")], [R("u7")])
+        tt(T.at[:, c8], T.u7[:, c8], T.i8[:, c8], ALU.add, [R("u7"), A_("i8")], [R("at")])
+
+    def sub(lst, other, ch):
+        lo, w0 = 1024 * ch, 64 * ch
+        op("v", lambda: vec.tensor_tensor(T.d[:, lo:lo + 1024], T.xv[:, 0:V].indirect(T[lst][:, w0:w0 + 64]), T[other][:, lo:lo + 1024], ALU.subtract),
+           [A_("xv"), A_(lst, w0, w0 + 64), A_(other, lo, lo + 1024)], [A_("d", lo, lo + 1024)])
+
+    def size(ch):
+        lo = 1024 * ch
+        actv(T.ad[:, 4 * ch:4 * ch + 4, :], T.d[:, lo:lo + 1024], ACT.Abs, [A_("d", lo, lo + 1024)], [A_("ad", lo, lo + 1024)])
+
+    def pe_sum(ch, least):
+        P, k = "P%d" % (ch // 2), ch % 2
+        o = (128 if least else 256) + 64 * k
+        out = T[P][:, o:o + 64]
+        E = "ED" if least else "EZ"
+        if least:
+            mm(out, T.ones[0:1, :], T.jrow[0:1, :], True, False, [A_("ones"), A_("jrow")], [A_(P)])
+        for b in range(16):
+            mm(out, T[E][:, 15 - b:143 - b], T.ad[:, 4 * ch:4 * ch + 4, 16 * b:16 * b + 16], b == 0 and not least, b == 15,
+               [A_(E), A_("ad", 1024 * ch, 1024 * ch + 1024)], [A_(P)])
+
+    def pe_rtab(h):
+        RW = A_("r16", 128 * h, 128 * h + 128)
+        for q4 in range(4):
+            e = nextbank()
+            for j in range(4):
+                c, rc = cmat(4 * q4 + j, 0)
+                mm(T[e][:, 128 * j:128 * j + 128], c, T.r16[:, 128 * h:128 * h + 128], True, True, [rc, RW], [A_(e)])
+            lo = 2048 * h + 512 * q4
+            actv(T.RTab[:, lo:lo + 512], T[e][:], ACT.Copy, [A_(e)], [A_("RTab", lo, lo + 512)])
+
+    def least(t, h):
+        P = "P%d" % h
+        c8, w = slice(8 * h, 8 * h + 8), slice(128 * h, 128 * h + 128)
+        R = lambda b: A_(b, 8 * h, 8 * h + 8)
+        RW = lambda b: A_(b, 128 * h, 128 * h + 128)
+        op("v", lambda: vec.tensor_tensor_scan(T.km[:, w], T.rs[:], T[P][:, 128:256], 0.0, ALU.max, ALU.min), [A_("rs"), A_(P)], [RW("km")])
+        tcopy(T.kk[:, c8], T.km[:, 128 * h + 15:128 * h + 128:16], [RW("km")], [R("kk")])
+        if t < NRT:
+            ts(T.ks[:, c8], T.kk[:, c8], 15360, 3, ALU.bitwise_and, ALU.logical_shift_right, [R("kk")], [R("ks")])
+            tt(T.kq[:, c8], T.ks[:, c8], T.ili[:, 0:8], ALU.add, [R("ks"), A_("ili")], [R("kq")])
+            win, rw = T.RTab[:, 2048 * h:2048 * h + 2048], A_("RTab", 2048 * h, 2048 * h + 2048)
+        else:
+            ts(T.ks[:, c8], T.kk[:, c8], 15360, None, ALU.bitwise_and, None, [R("kk")], [R("ks")])
+            tt(T.kq[:, c8], T.ks[:, c8], T.cc[:, c8], ALU.add, [R("ks"), R("cc")], [R("kq")])
+            win, rw = T.RTR[:], A_("RTR")
+        tcopy(T.qo[:, c8], T.kq[:, c8], [R("kq")], [R("qo")])
+        tcopy(T.ql[:, w], win.indirect(T.qo[:, c8]), [rw, R("qo")], [RW("ql")])
+
+    def misc(h):
+        L = "L%d" % h
+        w = slice(128 * h, 128 * h + 128)
+        RW = lambda b: A_(b, 128 * h, 128 * h + 128)
+        tcopy(T.q16[:, w], T.ql[:, w], [RW("ql")], [RW("q16")])
+        ts(T.n16[:, w], T.ql[:, w], 0.5, 1023.8, ALU.mult, ALU.add, [RW("ql")], [RW("n16")])
+        mm(T[L][:, 128:256], T.I4[:], T.n16[:, w], True, False, [A_("I4"), RW("n16")], [A_(L)])
+        mm(T[L][:, 128:256], T.IM[:], T.q16[:, w], False, True, [A_("IM"), RW("q16")], [A_(L)])
+        tcopy(T.uli[:, w], T[L][:, 0:128], [A_(L)], [RW("uli")])
+        ts(T.ulm[:, w], T.uli[:, w], 4095, None, ALU.bitwise_and, None, [RW("uli")], [RW("ulm")])
+        ts(T.ul[:, w], T.ulm[:, w], 32.0, None, ALU.add, None, [RW("ulm")], [RW("ul")])
+        tt(T.zi[:, w], T.q16[:, w], T.ul[:, w], ALU.mult, [RW("q16"), RW("ul")], [RW("zi")])
+        ts(T.hi[:, w], T.zi[:, w], 5, 2047, ALU.logical_shift_right, ALU.bitwise_and, [RW("zi")], [RW("hi")])
+        tcopy(T.h16[:, w], T.hi[:, w], [RW("hi")], [RW("h16")])
+        ts(T.qc[:, w], T[L][:, 128:256], -4095.0, None, ALU.add, None, [A_(L)], [RW("qc")])
+
+    def pe_new(h, lens, rho):
+        e = nextbank()
+        w = slice(128 * h, 128 * h + 128)
+        RW = lambda b: A_(b, 128 * h, 128 * h + 128)
+        for j, l in enumerate(lens):
+            if l < 10:
+                parts = [(l + 1, "w16")]
+            elif l == 16:
+                parts = [(0, "h16")]
+            else:
+                parts = [(MW + l - 10, "w16"), (MQ + l - 10, "qc"), (MH + l - 10, "h16")]
+            for k, (m, src) in enumerate(parts):
+                c, rc = cmat(m, rho)
+                mm(T[e][:, 128 * j:128 * j + 128], c, T[src][:, w], k == 0, k == len(parts) - 1, [rc, RW(src)], [A_(e)])
+        return e
+
+    def evac(h, lens, e):
+        lo, sz = 2176 * h + 128 * lens[0], 128 * len(lens)
+        actv(T.NT[:, lo:lo + sz], T[e][:, 0:sz], ACT.Copy, [A_(e)], [A_("NT", lo, lo + sz)])
+
+    def match(h):
+        P = "P%d" % h
+        c8, w = slice(8 * h, 8 * h + 8), slice(128 * h, 128 * h + 128)
+        R = lambda b: A_(b, 8 * h, 8 * h + 8)
+        RW = lambda b: A_(b, 128 * h, 128 * h + 128)
+        tt(T.okb[:, w], T[P][:, 256:384], T.THe[:], ALU.is_le, [A_(P), A_("THe")], [RW("okb")])
+        op("v", lambda: vec.tensor_tensor_scan(T.hs[:, w], T.okb[:, w], T.ones[:], 1.0, ALU.mult, ALU.add),
+           [RW("okb"), A_("ones")], [RW("hs")])
+        ts(T.fm[:, c8], T.hs[:, 128 * h + 15:128 * h + 128:16], 17.0, 128.0, ALU.min, ALU.mult, [RW("hs")], [R("fm")])
+        tt(T.fo[:, c8], T.fm[:, c8], T.ilc[:, 0:8], ALU.add, [R("fm"), A_("ilc")], [R("fo")])
+
+    def pe_list(h, rho):
+        P = "P%d" % h
+        mm(T[P][:, 384:392], T.rot[:, rho, :], T.fo[:, 8 * h:8 * h + 8], True, True, [A_("rot", rho, rho + 1), A_("fo", 8 * h, 8 * h + 8)], [A_(P)])
+
+    def final(t, h):
+        c8, w = slice(8 * h, 8 * h + 8), slice(128 * h, 128 * h + 128)
+        R = lambda b: A_(b, 8 * h, 8 * h + 8)
+        P = "P%d" % h
+        rho = GSH[t]
+        if rho:
+            pe_list(h, rho)
+
+    def final2(t, h):
+        c8, w = slice(8 * h, 8 * h + 8), slice(128 * h, 128 * h + 128)
+        R = lambda b: A_(b, 8 * h, 8 * h + 8)
+        P = "P%d" % h
+        if GSH[t]:
+            tcopy(T.fl[:, c8], T[P][:, 384:392], [A_(P)], [R("fl")])
+        else:
+            tcopy(T.fl[:, c8], T.fo[:, c8], [R("fo")], [R("fl")])
+        out = "S%d" % t if t < NV - 1 else "yf"
+        lo = 2176 * h
+        tcopy(T[out][:, w], T.NT[:, lo:lo + 2176].indirect(T.fl[:, c8]), [A_("NT", lo, lo + 2176), R("fl")], [A_(out, 128 * h, 128 * h + 128)])
+        if t < NV - 1:
+            deps("g", [A_(out, 128 * h, 128 * h + 128)], [])
+            rid, pid = topo.addr(nxt, core)
+            g.remote_dma(T["W%d" % (t + 1)][:, w], T[out][:, w], T.sem["ar%d_%d" % (t + 1, h)], T.sem.ls, pid, rid, smask)
+
+    def eng_mask(src, dst):
+        return sum(1 << e for e in topo.engines(src, dst)[:8])
+
+    smask = eng_mask(core, nxt)
+    n_in = len(topo.engines(prv, core)[:8])
+    n_out = len(topo.engines(core, nxt)[:8])
+
+    def pe_nv(h):
+        L, lo = "L%d" % h, 2048 * h
+        rx, rd = A_("xw", lo, lo + 2048), A_("d", lo, lo + 2048)
+        out = T[L][:, 256:384]
+        mm(out, T.IB[:], T.xw[:, lo + 15:lo + 2048:16], True, False, [rx, A_("IB")], [A_(L)])
+        mm(out, T.IB[:], T.xw[:, lo:lo + 2048:16], False, False, [rx, A_("IB")], [A_(L)])
+        mm(out, T.IB[:], T.d[:, lo:lo + 2048:16], False, True, [rd, A_("IB")], [A_(L)])
+
+    def new_values(h):
+        L, w = "L%d" % h, slice(128 * h, 128 * h + 128)
+        ts(T.nv[:, w], T[L][:, 256:384], 0.5, -0.25, ALU.mult, ALU.add, [A_(L)], [A_("nv", 128 * h, 128 * h + 128)])
+
+    def write_list(h):
+        c8 = slice(8 * h, 8 * h + 8)
+        R = lambda b: A_(b, 8 * h, 8 * h + 8)
+        ts(T.yb[:, c8], T.fo[:, c8], -8192.0, 10481664.0, ALU.mult, ALU.add, [R("fo")], [R("yb")])
+        tt(T.s1[:, c8], T.yb[:, c8], T.dm[:, c8], ALU.min, [R("yb"), A_("dm")], [R("s1")])
+        tt(T.s2[:, c8], T.s1[:, c8], T.at[:, c8], ALU.max, [R("s1"), R("at")], [R("s2")])
+        tcopy(T.sl[:, c8], T.s2[:, c8], [R("s2")], [R("sl")])
+
+    def scatter():
+        tcopy(T.xv[:].indirect(T.sl[:]), T.nv[:], [A_("sl"), A_("nv")], [A_("xv")])
+
+    def count():
+        for h in range(2):
+            c8 = slice(8 * h, 8 * h + 8)
+            ts(T.rp[:, c8], T.fo[:, c8], 1280.0, None, ALU.is_ge, None, [A_("fo", 8 * h, 8 * h + 8)], [A_("rp", 8 * h, 8 * h + 8)])
+        mm(T.P0[:, 400:416], T.ones[:], T.rp[:], True, True, [A_("ones"), A_("rp")], [A_("P0")])
+        actv(T.aj[:], T.P0[:, 400:416], ACT.Copy, [A_("P0")], [A_("aj"), A_("ac")], accum_out=T.ac[:, 0:1])
+
+    def allowance():
+        tcopy(T.aci[:, 0:1], T.ac[:, 0:1], [A_("ac")], [A_("aci")])
+        ts(T.acm[:, 0:1], T.aci[:, 0:1], 31, None, ALU.bitwise_and, None, [A_("aci")], [A_("acm")])
+        ts(T.a8[:, 0:1], T.acm[:, 0:1], 8.0, None, ALU.mult, None, [A_("acm")], [A_("a8")])
+        ts(T.THe[:], T.TH[:], T.a8[:, 0:1], None, ALU.add, None, [A_("TH"), A_("a8")], [A_("THe")])
+
+    for t in range(1, NV):
+        for h in range(2):
+            acc.setdefault("W%d" % t, []).append([128 * h, 128 * h + 128, "remote", ("ar%d_%d" % (t, h), n_in), True])
+
+    for t in range(NV):
+        rho = GSH[t]
+        G = [[0, 1, 2, 3], [4, 5, 6, 7], [8, 9, 10, 11], [12, 13, 14, 15], [16]]
+        W = "W%d" % t
+        gather_values("s", t, 0, 64)
+        gather_values("v", t, 64, 128)
+        pe_u(0)
+        gather_values("s", t, 128, 256)
+        expand(0)
+        tcopy(T.w16[:, 0:128], T[W][:, 0:128], [A_(W, 0, 128)], [A_("w16", 0, 128)])
+        relators(t, 0)
+        turned = {}
+        turned[(0, 0)] = pe_new(0, G[0], rho)
+        turned[(0, 1)] = pe_new(0, G[1], rho)
+        pe_u(1)
+        sub("rl", "X0", 0)
+        evac(0, G[0], turned[(0, 0)])
+        size(0)
+        sub("rl", "X0", 1)
+        evac(0, G[1], turned[(0, 1)])
+        size(1)
+        tcopy(T.w16[:, 128:256], T[W][:, 128:256], [A_(W, 128, 256)], [A_("w16", 128, 256)])
+        expand(1)
+        relators(t, 1)
+        pe_sum(0, True)
+        pe_sum(1, True)
+        if t < NRT:
+            pe_rtab(0)
+        turned[(1, 0)] = pe_new(1, G[0], rho)
+        turned[(1, 1)] = pe_new(1, G[1], rho)
+        sub("rl", "X0", 2)
+        evac(1, G[0], turned[(1, 0)])
+        size(2)
+        if t == 0:
+            late_constants()
+            tcopy(T.THe[:], T.TH[:], [A_("TH")], [A_("THe")])
+        else:
+            allowance()
+        least(t, 0)
+        sub("rl", "X0", 3)
+        evac(1, G[1], turned[(1, 1)])
+        size(3)
+        pe_sum(2, True)
+        pe_sum(3, True)
+        if t < NRT:
+            pe_rtab(1)
+        sub("ql", "xw", 0)
+        size(0)
+        at_list(0)
+        at_list(1)
+        misc(0)
+        sub("ql", "xw", 1)
+        size(1)
+        pe_sum(0, False)
+        pe_sum(1, False)
+        pe_nv(0)
+        e2 = pe_new(0, G[2], rho)
+        e3 = pe_new(0, G[3], rho)
+        e4 = pe_new(0, G[4], rho)
+        least(t, 1)
+        sub("ql", "xw", 2)
+        evac(0, G[2], e2)
+        evac(0, G[3], e3)
+        size(2)
+        evac(0, G[4], e4)
+        misc(1)
+        sub("ql", "xw", 3)
+        size(3)
+        pe_sum(2, False)
+        f2 = pe_new(1, G[2], rho)
+        pe_sum(3, False)
+        pe_nv(1)
+        f3 = pe_new(1, G[3], rho)
+        f4 = pe_new(1, G[4], rho)
+        evac(1, G[2], f2)
+        evac(1, G[3], f3)
+        evac(1, G[4], f4)
+        match(0)
+        final(t, 0)
+        new_values(0)
+        write_list(0)
+        final2(t, 0)
+        match(1)
+        final(t, 1)
+        new_values(1)
+        write_list(1)
+        scatter()
+        final2(t, 1)
+        if t < NV - 1:
+            count()
+
+    dma("y", T.yx[:], T.xv[:, 0:V], [A_("xv")], [], "out0", 16)
+    c, rc = cmat(REV, 0)
+    mm(T.E0[:, 0:256], c, T.yf[:], True, True, [rc, A_("yf")], [A_("E0")])
+    tcopy(T.yo[:], T.E0[:, 0:256], [A_("E0")], [A_("yo")])
+    dma("s", T.yw[:], T.yo[:], [A_("yo")], [], "out1", 16)
+    for q in ("v", "s", "t", "g"):
+        need("g", ("q" + q, cnt[q]))
+    for k in range(6):
+        need("g", ("ld%d" % k, 16))
+    need("g", ("rd", 32))
+    need("g", ("rtl", 256))
+    for t in range(1, NV):
+        for h in range(2):
+            need("g", ("ar%d_%d" % (t, h), n_in))
+    need("g", ("ls", 2 * (NV - 1) * n_out))
+    need("g", ("out0", 16))
+    need("g", ("out1", 16))

@@ -5,69 +5,103 @@ ALU = AluOpType
 ACT = ActivationFunctionType
 NV = 5
 NRT = 1
+CHW = 64
+XCH = 64
+MISC = ((0, 128), (128, 256))
 NM = 35
 MQ, MW, MH, REV = 16, 22, 28, 34
 V = 2048
+LOOK = 0.05
+PEC = 0.0008
 
-SCRATCH = {
-    "xv": ("sbuf", [128, 2304], "bfloat16"),
-    "wdi": ("sbuf", [128, 256], "int32"), "rti": ("sbuf", [128, 1024], "int32"),
-    "wti": ("sbuf", [128, 8], "int32"), "thi": ("sbuf", [128, 8], "int32"),
-    "wd16": ("sbuf", [128, 256], "float16"), "rt16": ("sbuf", [128, 1024], "float16"),
-    "RT0": ("sbuf", [128, 1024], "float32"),
-    "RTR": ("sbuf", [128, 16384], "float32"), "RD": ("dram", [8, 32, 1024], "float32"),
-    "RTab": ("sbuf", [128, 4096], "float32"), "NT": ("sbuf", [128, 2 * 17 * 128], "float32"),
-    "W0": ("sbuf", [128, 256], "uint16"), "W1": ("sbuf", [128, 256], "uint16"), "W2": ("sbuf", [128, 256], "uint16"),
-    "W3": ("sbuf", [128, 256], "uint16"), "W4": ("sbuf", [128, 256], "uint16"),
-    "S0": ("sbuf", [128, 256], "uint16"), "S1": ("sbuf", [128, 256], "uint16"), "S2": ("sbuf", [128, 256], "uint16"),
-    "S3": ("sbuf", [128, 256], "uint16"),
-    "w16": ("sbuf", [128, 256], "float16"),
-    "xw": ("sbuf", [128, 4096], "bfloat16"), "Z": ("sbuf", [128, 4096], "bfloat16"), "X0": ("sbuf", [128, 4096], "bfloat16"),
-    "d": ("sbuf", [128, 4096], "bfloat16"), "ad": ("sbuf", [128, 16, 256], "bfloat16"),
-    "hold": ("sbuf", [128, 2048], "bfloat16"),
-    "row": ("sbuf", [128, 144], "int32"), "grow": ("sbuf", [128, 128], "int32"), "krow": ("sbuf", [128, 128], "int32"),
-    "pc": ("sbuf", [128, 8], "int32"), "ai": ("sbuf", [128, 16], "int32"), "gam": ("sbuf", [128, 16], "int32"),
-    "ki": ("sbuf", [128, 8], "int32"), "gi": ("sbuf", [128, 8], "int32"),
-    "pf": ("sbuf", [128, 8], "float32"), "kf": ("sbuf", [128, 8], "float32"), "gf": ("sbuf", [128, 8], "float32"),
-    "g16": ("sbuf", [128, 8], "float32"), "whi_i": ("sbuf", [128, 8], "int32"), "wlo_i": ("sbuf", [128, 8], "int32"),
-    "whi": ("sbuf", [128, 8], "float32"), "wlo": ("sbuf", [128, 8], "float32"), "thf": ("sbuf", [128, 8], "float32"),
-    "kr15": ("sbuf", [128, 8], "float32"), "bm": ("sbuf", [128, 16], "float32"),
-    "tgt": ("sbuf", [128, 560], "int32"), "tga": ("sbuf", [128, 256], "int32"),
-    "F1": ("sbuf", [128, 35, 16], "bfloat16"), "CM": ("sbuf", [128, 35, 160], "bfloat16"),
-    "EZ": ("sbuf", [128, 144], "bfloat16"), "ED": ("sbuf", [128, 144], "bfloat16"),
-    "WZh": ("sbuf", [128, 144], "bfloat16"), "WZl": ("sbuf", [128, 144], "bfloat16"),
-    "WBh": ("sbuf", [128, 128], "bfloat16"), "WBl": ("sbuf", [128, 128], "bfloat16"),
-    "BO": ("sbuf", [128, 128], "float32"), "thr": ("sbuf", [128, 128], "float32"),
-    "IB": ("sbuf", [128, 128], "bfloat16"), "I4": ("sbuf", [128, 128], "bfloat16"), "IM": ("sbuf", [128, 128], "bfloat16"),
-    "rot": ("sbuf", [128, 3, 128], "float32"),
-    "ones": ("sbuf", [128, 128], "bfloat16"), "jrow": ("sbuf", [128, 64], "bfloat16"), "rs": ("sbuf", [128, 128], "float32"),
-    "okb": ("sbuf", [128, 256], "bfloat16"), "hs": ("sbuf", [128, 256], "bfloat16"), "ilc": ("sbuf", [128, 16], "float32"),
-    "fm": ("sbuf", [128, 16], "float32"), "yb": ("sbuf", [128, 16], "float32"),
-    "ilf": ("sbuf", [128, 16], "float32"), "ili": ("sbuf", [128, 16], "int32"), "i8": ("sbuf", [128, 16], "float32"),
-    "dm": ("sbuf", [128, 16], "float32"), "TH": ("sbuf", [128, 128], "float32"), "THe": ("sbuf", [128, 128], "float32"),
-    "ui": ("sbuf", [128, 16], "int32"), "uu": ("sbuf", [128, 16], "int32"), "tf": ("sbuf", [128, 16], "float32"),
-    "zz": ("sbuf", [128, 16], "int32"), "cc": ("sbuf", [128, 16], "int32"), "cl": ("sbuf", [128, 16], "uint16"),
-    "u7": ("sbuf", [128, 16], "int32"), "at": ("sbuf", [128, 16], "float32"), "km": ("sbuf", [128, 256], "float32"),
-    "kk": ("sbuf", [128, 16], "int32"), "ks": ("sbuf", [128, 16], "int32"), "kq": ("sbuf", [128, 16], "int32"),
-    "qo": ("sbuf", [128, 16], "uint16"), "rl": ("sbuf", [128, 256], "uint16"), "ql": ("sbuf", [128, 256], "uint16"),
-    "r16": ("sbuf", [128, 256], "float16"),
-    "q16": ("sbuf", [128, 256], "float16"), "n16": ("sbuf", [128, 256], "float16"), "qc": ("sbuf", [128, 256], "float16"),
-    "uli": ("sbuf", [128, 256], "int32"), "ulm": ("sbuf", [128, 256], "int32"), "ul": ("sbuf", [128, 256], "float32"),
-    "zi": ("sbuf", [128, 256], "int32"), "hi": ("sbuf", [128, 256], "int32"), "h16": ("sbuf", [128, 256], "float16"),
-    "fo": ("sbuf", [128, 16], "float32"), "fl": ("sbuf", [128, 16], "uint16"), "rp": ("sbuf", [128, 16], "bfloat16"),
-    "s1": ("sbuf", [128, 16], "float32"), "s2": ("sbuf", [128, 16], "float32"), "sl": ("sbuf", [128, 16], "uint16"),
-    "nv": ("sbuf", [128, 256], "int32"), "aj": ("sbuf", [128, 16], "float32"), "ac": ("sbuf", [128, 8], "float32"),
-    "aci": ("sbuf", [128, 8], "int32"), "acm": ("sbuf", [128, 8], "int32"), "a8": ("sbuf", [128, 8], "float32"),
-    "yf": ("sbuf", [128, 256], "float16"), "yo": ("sbuf", [128, 256], "float32"),
-    "P0": ("psum", [128, 512], "float32"), "P1": ("psum", [128, 512], "float32"),
-    "L0": ("psum", [128, 512], "float32"), "L1": ("psum", [128, 512], "float32"),
-    "E0": ("psum", [128, 512], "float32"), "E1": ("psum", [128, 512], "float32"),
-    "E2": ("psum", [128, 512], "float32"), "E3": ("psum", [128, 512], "float32"),
-}
+f32, bf, fp, i32, u16 = "float32", "bfloat16", "float16", "int32", "uint16"
+SCRATCH = {"RD": ("dram", [8, 32, 1024], f32)}
+for names, shape, d in (
+        ("xv", [128, 4096], bf), ("wdi", [128, 256], i32), ("rti", [128, 1024], i32), ("wti thi", [128, 8], i32),
+        ("wd16", [128, 256], fp), ("rt16", [128, 1024], fp), ("RT0", [128, 1024], f32), ("RTR", [128, 16384], f32),
+        ("RTab", [128, 4096], f32), ("NT", [128, 4352], f32), ("W0 W1 W2 W3 W4 S0 S1 S2 S3 rl ql", [128, 256], u16),
+        ("w16 r16 q16 n16 qc h16 yf", [128, 256], fp), ("zi hi nv", [128, 256], i32),
+        ("xw X0 d", [128, 4096], bf), ("ad", [128, 16, 256], bf), ("Z hold", [128, 2048], bf),
+        ("row", [128, 144], i32), ("grow krow", [128, 128], i32), ("pc ki gi whi_i wlo_i aci acm", [128, 8], i32),
+        ("ai gam", [128, 16], i32), ("pf kf gf g16 whi wlo thf kr15 ac a8", [128, 8], f32), ("bm oh", [128, 16], f32),
+        ("tgt", [128, 560], i32), ("tga", [128, 256], i32), ("F1", [128, 35, 16], bf), ("CM", [128, 35, 160], bf),
+        ("EZ ED WZh WZl", [128, 144], bf), ("BOb IB I4 IM ones", [128, 128], bf), ("c32", [128, 256], bf), ("BB", [128, 16, 128], bf),
+        ("BO thr rs TH THe", [128, 128], f32), ("jrow", [128, 64], bf), ("okb hs", [128, 256], bf), ("km yo", [128, 256], f32),
+        ("ilf i8 tf at n2 s2 aj", [128, 16], f32), ("ilc fm rp", [128, 16], bf), ("uh ulo", [128, 16], fp),
+        ("ili ui uu zz cc u7 kk ks kq", [128, 16], i32), ("cl qo fl sl", [128, 16], u16)):
+    for _n in names.split():
+        SCRATCH[_n] = ("sbuf", shape, d)
 PSUM = ("P0", "P1", "L0", "L1", "E0", "E1", "E2", "E3")
-SEMAPHORES = (["qv", "qs", "qt", "qg", "ls"] + ["ld%d" % k for k in range(8)] + ["rd", "rtl", "out0", "out1"]
+for _n in PSUM:
+    SCRATCH[_n] = ("psum", [128, 512], f32)
+SEMAPHORES = (["qv", "qs", "qt", "qg", "ls"] + ["ld%d" % k for k in range(6)] + ["rd", "rtl", "out0", "out1"]
               + ["ar%d_%d" % (t, h) for t in range(1, NV) for h in range(2)])
 GSH = [(t + t // 4) - (t - 1 + (t - 1) // 4) for t in range(1, NV)] + [0]
+
+
+def schedule(ops):
+    wake, hist, n = 0.1, {}, len(ops)
+    preds, succs = [{} for _ in ops], [[] for _ in ops]
+    for i, o in enumerate(ops):
+        q = o["q"]
+        for regs, wr in ((o["r"], False), (o["w"], True)):
+            for b, lo, hi in regs:
+                for l2, h2, j, w2 in hist.get(b, ()):
+                    if j == i or (b not in PSUM and (l2 >= hi or h2 <= lo or not (wr or w2))):
+                        continue
+                    lat = wake if (ops[j]["q"] != q or b not in PSUM or ops[j]["lat"]) else 0.0
+                    preds[i][j] = max(preds[i].get(j, 0.0), lat)
+        for regs, wr in ((o["r"], False), (o["w"], True)):
+            for b, lo, hi in regs:
+                if b in PSUM:
+                    hist[b] = [(lo, hi, i, True)]
+                else:
+                    old = hist.get(b, [])
+                    if wr:
+                        old = [e for e in old if not (e[0] >= lo and e[1] <= hi)]
+                    hist[b] = old + [(lo, hi, i, wr)]
+    for i in range(n):
+        for j, lat in preds[i].items():
+            succs[j].append((i, lat))
+    prio = [0.0] * n
+    for i in range(n - 1, -1, -1):
+        prio[i] = ops[i]["cost"] + ops[i]["lat"] + max([prio[j] + lat for j, lat in succs[i]] + [0.0])
+    left = [len(p) for p in preds]
+    ready = [0.0] * n
+    cand = {}
+
+    def enter(i):
+        for q in (("s", "v") if ops[i]["q"] == "vs" else (ops[i]["q"],)):
+            cand.setdefault(q, []).append(i)
+
+    for i in range(n):
+        if not left[i]:
+            enter(i)
+    free, order = {}, []
+    while len(order) < n:
+        best = None
+        for q, c in cand.items():
+            if not c:
+                continue
+            t0 = min(max(free.get(q, 0.0), ready[i]) for i in c)
+            k = max((i for i in c if max(free.get(q, 0.0), ready[i]) <= t0 + LOOK), key=lambda i: (prio[i], -i))
+            st = max(free.get(q, 0.0), ready[k])
+            if best is None or st < best[0]:
+                best = (st, k, q)
+        st, i, q = best
+        for c in cand.values():
+            if i in c:
+                c.remove(i)
+        if ops[i]["q"] == "vs":
+            ops[i]["q"], ops[i]["f"] = q, ops[i]["f"][q]
+        free[q] = st + ops[i]["cost"]
+        order.append(i)
+        for j, lat in succs[i]:
+            ready[j] = max(ready[j], free[q] + ops[i]["lat"] + lat)
+            left[j] -= 1
+            if not left[j]:
+                enter(j)
+    return order
 
 
 def rank_program(g, core, T, topo):
@@ -76,12 +110,390 @@ def rank_program(g, core, T, topo):
         return
     n = len(T.cores)
     nxt, prv = T.cores[(rank + 1) % n], T.cores[(rank - 1) % n]
+    out_engines = topo.engines(core, nxt)[:8]
+    smask, n_out = sum(1 << e for e in out_engines), len(out_engines)
+    n_in = len(topo.engines(prv, core)[:8])
+
+    ops = []
+
+    def op(q, fns, r, w, cost, lat=0.0, kind="c", sem=None):
+        ops.append({"q": q, "f": fns, "r": r, "w": w, "cost": cost, "lat": lat, "kind": kind, "sem": sem})
+
+    CY = 0.00083
+    A_ = lambda b, lo=0, hi=1 << 20: (b, lo, hi)
+    vec, sca, ten = g.vector, g.scalar, g.tensor
+
+    def tcopy(out, in_, r, w, k=256):
+        op("v", [lambda: vec.tensor_copy(out, in_)], r, w, 0.06 + CY * max(64, k))
+
+    def vgather(out, win, off, r, w, k):
+        op("v", [lambda: vec.tensor_copy(out, win.indirect(off))], r, w, 0.06 + 1.5 * CY * k)
+
+    def tt(out, a, b, o, r, w, k=64):
+        op("v", [lambda: vec.tensor_tensor(out, a, b, o)], r, w, 0.06 + CY * max(64, k))
+
+    def ts(out, a, s1, s2, o0, o1, r, w, k=64):
+        if o1 is None:
+            op("v", [lambda: vec.tensor_scalar(out, a, s1, None, o0)], r, w, 0.06 + CY * max(64, k))
+        else:
+            op("v", [lambda: vec.tensor_scalar(out, a, s1, s2, o0, o1)], r, w, 0.06 + CY * max(64, k))
+
+    def scan(out, d0, d1, init, o0, o1, r, w, k):
+        op("v", [lambda: vec.tensor_tensor_scan(out, d0, d1, init, o0, o1)], r, w, 0.06 + CY * k)
+
+    def mset(ap, c, w, k, r=()):
+        op("v", [lambda: vec.memset(ap, c)], list(r), w, 0.06 + CY * max(64, k))
+
+    def actv(out, in_, f, r, w, k, **kw):
+        op("s", [lambda: sca.activation(out, in_, f, **kw)], r, w, 0.18 + CY * k)
+
+    def mms(lst, r, w, cols=64):
+        op("t", [(lambda a: lambda: ten.matmul(*a))(a) for a in lst], r, w, len(lst) * PEC * cols)
+
+    def iota(out, pat, base, cm, w, k=16):
+        op("g", [lambda: g.iota(out, pat, base, cm)], [], w, 0.13 + 2 * CY * k)
+
+    def dma(q, out, in_, r, w, sem, total, lat):
+        eng = {"y": g.sync, "s": sca}[q]
+        op(q, [lambda: eng.dma_start(out, in_)], r, w, 0.07, lat, "d", (sem, total))
+
+    dma("s", T.wdi[:], T.wd[:], [], [A_("wdi")], "ld0", 16, 2.5)
+    dma("y", T.xv[:, 0:V], T.x[:], [], [A_("xv", 0, V)], "ld1", 16, 5.0)
+    dma("s", T.rti[:, 712:1024], T.rt[:, 0:312], [], [A_("rti", 712, 1024)], "ld2", 16, 4.0)
+    dma("s", T.rti[:, 0:712], T.rt[:, 312:1024], [], [A_("rti", 0, 712)], "ld3", 16, 5.0)
+    dma("s", T.wti[:, 0:1], T.wt[:], [], [A_("wti")], "ld4", 16, 4.0)
+    dma("s", T.thi[:, 0:1], T.th[:], [], [A_("thi")], "ld5", 16, 5.0)
+
+    iota(T.pc[:, 0:1], [[1, 1]], 0, 1, [A_("pc")])
+    iota(T.tga[:], [[-1, 16], [1, 16]], 16, 0, [A_("tga")], 256)
+    iota(T.gam[:, 0:10], [[1, 10]], 6, 0, [A_("gam")])
+    mset(T.tgt[:, 256:560], -1, [A_("tgt", 256, 560)], 304)
+    iota(T.tgt[:, REV * 16:REV * 16 + 16], [[-1, 16]], 15, 0, [A_("tgt", REV * 16, REV * 16 + 16)])
+    for l in range(10, 16):
+        a = (MQ + l - 10) * 16
+        iota(T.tgt[:, a + l:a + 16], [[-1, 16 - l]], 15 - l, 0, [A_("tgt", a + l, a + 16)])
+        a = (MW + l - 10) * 16
+        iota(T.tgt[:, a + 2 * l - 16:a + l], [[1, 16 - l]], 0, 0, [A_("tgt", a + 2 * l - 16, a + l)])
+        a = (MH + l - 10) * 16
+        iota(T.tgt[:, a:a + 2 * l - 16], [[1, 2 * l - 16]], 0, 0, [A_("tgt", a, a + 2 * l - 16)])
+    iota(T.row[:, 0:144], [[1, 144]], 0, 0, [A_("row")], 144)
+    iota(T.grow[:], [[1, 8], [0, 16]], 0, 0, [A_("grow")], 128)
+    iota(T.krow[:], [[0, 8], [1, 16]], 0, 0, [A_("krow")], 128)
+    iota(T.ai[:], [[16, 16]], 0, 0, [A_("ai")])
+
+    ts(T.ki[:, 0:1], T.pc[:, 0:1], 15, None, ALU.bitwise_and, None, [A_("pc")], [A_("ki")])
+    ts(T.gi[:, 0:1], T.pc[:, 0:1], 4, None, ALU.logical_shift_right, None, [A_("pc")], [A_("gi")])
+    tcopy(T.pf[:, 0:1], T.pc[:, 0:1], [A_("pc")], [A_("pf")], 1)
+    tcopy(T.kf[:, 0:1], T.ki[:, 0:1], [A_("ki")], [A_("kf")], 1)
+    tcopy(T.gf[:, 0:1], T.gi[:, 0:1], [A_("gi")], [A_("gf")], 1)
+    ts(T.g16[:, 0:1], T.gf[:, 0:1], 16.0, 15.0, ALU.mult, ALU.add, [A_("gf")], [A_("g16")])
+    ts(T.kr15[:, 0:1], T.kf[:, 0:1], -1.0, 15.0, ALU.mult, ALU.add, [A_("kf")], [A_("kr15")])
+    ts(T.tgt[:, 0:256], T.tga[:], 15, None, ALU.bitwise_and, None, [A_("tga")], [A_("tgt", 0, 256)], 256)
+    ts(T.gam[:, 0:10], T.gam[:, 0:10], 7, None, ALU.bitwise_and, None, [A_("gam")], [A_("gam")])
+    ts(T.bm[:, 0:10], T.gam[:, 0:10], T.gf[:, 0:1], None, ALU.is_equal, None, [A_("gam"), A_("gf")], [A_("bm")])
+    for m0, m1 in ((34, 35), (0, 16), (16, 34)):
+        ts(T.F1[:, m0:m1, :], T.tgt[:, 16 * m0:16 * m1], T.kf[:, 0:1], None, ALU.is_equal, None,
+           [A_("tgt", 16 * m0, 16 * m1), A_("kf")], [A_("F1", m0, m1)], 16 * (m1 - m0))
+        for j in range(10):
+            o, i_, sc = T.CM[:, m0:m1, 16 * j:16 * j + 16], T.F1[:, m0:m1, :], T.bm[:, j:j + 1]
+            r, w = [A_("F1", m0, m1), A_("bm")], [A_("CM%d" % j, m0, m1)]
+            if m0 == 34 or (m0 == 16) == (j % 2 == 0):
+                ts(o, i_, sc, None, ALU.mult, None, r, w, 8 * (m1 - m0))
+            else:
+                actv(o, i_, ACT.Copy, r, w, 16 * (m1 - m0), scale=sc)
+
+    def cmat(m, rho):
+        lo = 16 * (2 - rho)
+        return T.CM[:, m, lo:lo + 128], [A_("CM%d" % j, m, m + 1) for j in range(2 - rho, 10 - rho)]
+
+    tcopy(T.wd16[:], T.wdi[:], [A_("wdi")], [A_("wd16")])
+    c, rc = cmat(REV, 0)
+    mms([(T.E0[:, 0:256], c, T.wd16[:], True, True)], rc + [A_("wd16")], [A_("E0")], 256)
+    tcopy(T.W0[:], T.E0[:, 0:256], [A_("E0")], [A_("W0")])
+    for k, e in ((0, "E1"), (1, "E2")):
+        s = slice(512 * k, 512 * k + 512)
+        tcopy(T.rt16[:, s], T.rti[:, s], [A_("rti", s.start, s.stop)], [A_("rt16", s.start, s.stop)], 512)
+        mms([(T[e][:], c, T.rt16[:, s], True, True)], rc + [A_("rt16", s.start, s.stop)], [A_(e)], 512)
+        actv(T.RT0[:, s], T[e][:], ACT.Copy, [A_(e)], [A_("RT0", s.start, s.stop)], 512)
+    dma("y", T.RD[:, 0:16, :], T.RT0[:], [A_("RT0")], [A_("RD", 0, 1)], "rd", 32, 5.0)
+    dma("y", T.RD[:, 16:32, :], T.RT0[:], [A_("RT0")], [A_("RD", 1, 2)], "rd", 32, 8.0)
+    for s in range(16):
+        dma("y", T.RTR[:, 1024 * s:1024 * s + 1024], T.RD[:, 16 - s:32 - s, :], [A_("RD")], [A_("RTR", s, s + 1)], "rtl", 256, 30.0)
+
+    ts(T.wlo_i[:, 0:1], T.wti[:, 0:1], 255, None, ALU.bitwise_and, None, [A_("wti")], [A_("wlo_i")])
+    ts(T.whi_i[:, 0:1], T.wti[:, 0:1], 3840, None, ALU.bitwise_and, None, [A_("wti")], [A_("whi_i")])
+    tcopy(T.wlo[:, 0:1], T.wlo_i[:, 0:1], [A_("wlo_i")], [A_("wlo")], 1)
+    tcopy(T.whi[:, 0:1], T.whi_i[:, 0:1], [A_("whi_i")], [A_("whi")], 1)
+    sel = [A_("row"), A_("g16")]
+    ts(T.WZh[:], T.row[:], T.g16[:, 0:1], T.whi[:, 0:1], ALU.is_equal, ALU.mult, sel + [A_("whi")], [A_("WZh")], 144)
+    ts(T.WZl[:], T.row[:], T.g16[:, 0:1], T.wlo[:, 0:1], ALU.is_equal, ALU.mult, sel + [A_("wlo")], [A_("WZl")], 144)
+    ts(T.ED[:], T.row[:], T.g16[:, 0:1], 16384.0, ALU.is_equal, ALU.mult, sel, [A_("ED")], 144)
+    ts(T.EZ[:], T.row[:], T.g16[:, 0:1], None, ALU.is_equal, None, sel, [A_("EZ")], 144)
+    mset(T.Z[:], 0.0, [A_("Z")], 1024)
+    mset(T.hold[:], 1.0, [A_("hold")], 1024)
+    mset(T.hold[:, 0:2048:16], 0.0, [A_("hold")], 64, [A_("hold")])
+    mset(T.ones[:], 1.0, [A_("ones")], 64)
+    mset(T.c32[:], 32.0, [A_("c32")], 64)
+    ts(T.jrow[:], T.krow[:, 0:64], -1024.0, 15360.0, ALU.mult, ALU.add, [A_("krow")], [A_("jrow")])
+    ts(T.rs[:], T.krow[:], 0.0, 1e9, ALU.is_equal, ALU.mult, [A_("krow")], [A_("rs")], 128)
+    ts(T.ilf[:], T.ai[:], T.kf[:, 0:1], None, ALU.add, None, [A_("ai"), A_("kf")], [A_("ilf")])
+    tcopy(T.ili[:], T.ilf[:], [A_("ilf")], [A_("ili")], 16)
+    ts(T.i8[:], T.ilf[:], 8.0, None, ALU.mult, None, [A_("ilf")], [A_("i8")])
+    ts(T.ilc[:, 0:8], T.ilf[:, 0:8], -128.0, None, ALU.add, None, [A_("ilf")], [A_("ilc")])
+    irow = T.row[:, 0:128]
+    ri = [A_("row"), A_("pf")]
+    ts(T.IB[:], irow, T.pf[:, 0:1], None, ALU.is_equal, None, ri, [A_("IB")], 128)
+    ts(T.I4[:], irow, T.pf[:, 0:1], 4.0, ALU.is_equal, ALU.mult, ri, [A_("I4")], 128)
+    ts(T.IM[:], irow, T.pf[:, 0:1], -1.0, ALU.is_equal, ALU.mult, ri, [A_("IM")], 128)
+    rg = [A_("grow"), A_("gf")]
+    ts(T.BO[:], T.grow[:], T.gf[:, 0:1], None, ALU.is_equal, None, rg, [A_("BO")], 128)
+    ts(T.BOb[:], T.grow[:], T.gf[:, 0:1], None, ALU.is_equal, None, rg, [A_("BOb")], 128)
+    ts(T.oh[:], T.krow[:, 0:16], T.kf[:, 0:1], None, ALU.is_equal, None, [A_("krow"), A_("kf")], [A_("oh")])
+    for b in range(16):
+        if b % 2:
+            ts(T.BB[:, b, :], T.BOb[:], T.oh[:, b:b + 1], None, ALU.mult, None, [A_("BOb"), A_("oh")], [A_("BB", b, b + 1)])
+        else:
+            actv(T.BB[:, b, :], T.BOb[:], ACT.Copy, [A_("BOb"), A_("oh")], [A_("BB", b, b + 1)], 128, scale=T.oh[:, b:b + 1])
+    tcopy(T.thf[:, 0:1], T.thi[:, 0:1], [A_("thi")], [A_("thf")], 1)
+    ts(T.thr[:], T.krow[:], T.kr15[:, 0:1], T.thf[:, 0:1], ALU.is_equal, ALU.mult, [A_("krow"), A_("kr15"), A_("thf")], [A_("thr")], 128)
+    mms([(T.L1[:, 0:128], T.BO[:], T.thr[:], True, True)], [A_("BO"), A_("thr")], [A_("L1")], 512)
+    tcopy(T.TH[:], T.L1[:, 0:128], [A_("L1")], [A_("TH")], 128)
+
+    ebank = [0]
+
+    def nextbank():
+        ebank[0] = (ebank[0] + 1) % 4
+        return "E%d" % ebank[0]
+
+    def T8(h):
+        return slice(8 * h, 8 * h + 8), (lambda b: A_(b, 8 * h, 8 * h + 8))
+
+    def L128(h):
+        return slice(128 * h, 128 * h + 128), (lambda b: A_(b, 128 * h, 128 * h + 128))
+
+    def values(t, h):
+        w = "W%d" % t
+        for ch in range(128 * h // XCH, 128 * (h + 1) // XCH):
+            lo, hi = ch * XCH, ch * XCH + XCH
+            r, wr = [A_("xv", 0, V), A_(w, lo, hi)], [A_("xw", 16 * lo, 16 * hi)]
+            out, win, off = T.xw[:, 16 * lo:16 * hi], T.xv[:, 0:V], T[w][:, lo:hi]
+            src = win.indirect(off)
+            op("vs", {"v": [(lambda o, s: lambda: vec.tensor_copy(o, s))(out, src)],
+                      "s": [(lambda o, s: lambda: sca.activation(o, s, ACT.Copy))(out, src)]}, r, wr, 0.1 + 24 * CY * XCH)
+
+    def u_sum(h):
+        P, lo = "P%d" % h, 2048 * h
+        l = []
+        for b in range(16):
+            rhs = T.xw[:, lo + 16 * b + 15:lo + 2048:256]
+            l.append((T[P][:, 0:8], T.WZh[:, 15 - b:143 - b], rhs, b == 0, False))
+            l.append((T[P][:, 0:8], T.WZl[:, 15 - b:143 - b], rhs, False, b == 15))
+        mms(l, [A_("xw", lo, lo + 2048), A_("WZh"), A_("WZl")], [A_(P)])
+
+    def expand(h):
+        lo = 2048 * h
+        R = lambda b: A_(b, lo, lo + 2048)
+        tcopy(T.Z[:, 0:2048:16], T.xw[:, lo + 15:lo + 2048:16], [R("xw")], [A_("Z")], 64)
+        scan(T.X0[:, lo:lo + 2048], T.hold[:], T.Z[:], 0.0, ALU.mult, ALU.add, [A_("hold"), A_("Z")], [R("X0")], 1024)
+
+    def relators(t, h):
+        P = "P%d" % h
+        c8, R = T8(h)
+        w, RW = L128(h)
+        tcopy(T.ui[:, c8], T[P][:, 0:8], [A_(P)], [R("ui")], 8)
+        ts(T.uu[:, c8], T.ui[:, c8], 4095, None, ALU.bitwise_and, None, [R("ui")], [R("uu")])
+        ts(T.tf[:, c8], T.uu[:, c8], 592.0, None, ALU.add, None, [R("uu")], [R("tf")])
+        tt(T.zz[:, c8], T.tf[:, c8], T.tf[:, c8], ALU.mult, [R("tf")], [R("zz")])
+        ts(T.cc[:, c8], T.zz[:, c8], 5, 1023, ALU.logical_shift_right, ALU.bitwise_and, [R("zz")], [R("cc")])
+        tcopy(T.cl[:, c8], T.cc[:, c8], [R("cc")], [R("cl")], 8)
+        vgather(T.rl[:, w], T.RT0[:], T.cl[:, c8], [A_("RT0"), R("cl")], [RW("rl")], 128)
+        if t < NRT:
+            tcopy(T.r16[:, w], T.rl[:, w], [RW("rl")], [RW("r16")], 64)
+
+    def spread_u():
+        tcopy(T.uh[:], T.uu[:], [A_("uu")], [A_("uh")], 16)
+        tt(T.ulo[:], T.uu[:], T.uh[:], ALU.subtract, [A_("uu"), A_("uh")], [A_("ulo")])
+        l = [(T.L0[:, 0:256], T.IB[:], T.c32[:], True, False)]
+        for b in range(16):
+            out = T.L0[:, b:256:16]
+            l.append((out, T.BB[:, b, :], T.uh[:], False, False))
+            l.append((out, T.BB[:, b, :], T.ulo[:], False, b == 15))
+        mms(l, [A_("IB"), A_("c32"), A_("BB"), A_("uh"), A_("ulo")], [A_("L0")])
+
+    def at_list():
+        ts(T.u7[:], T.ui[:], 7, None, ALU.bitwise_and, None, [A_("ui")], [A_("u7")])
+        tt(T.at[:], T.u7[:], T.i8[:], ALU.add, [A_("u7"), A_("i8")], [A_("at")])
+
+    def distances(lst, other, h, least):
+        P, W16 = "P%d" % h, 16 * CHW
+        for k in range(128 // CHW):
+            w0 = 128 * h + k * CHW
+            lo, hi, a0, a1 = 16 * w0, 16 * w0 + W16, w0 // 16, (w0 + CHW) // 16
+            d, win, off, x = T.d[:, lo:hi], T.xv[:, 0:V], T[lst][:, w0:w0 + CHW], T[other][:, lo:hi]
+            op("v", [(lambda d, win, off, x: lambda: vec.tensor_tensor(d, win.indirect(off), x, ALU.subtract))(d, win, off, x)],
+               [A_("xv", 0, V), A_(lst, w0, w0 + CHW), A_(other, lo, hi)], [A_("d", lo, hi)], 0.06 + 1.5 * CY * W16)
+            actv(T.ad[:, a0:a1, :], d, ACT.Abs, [A_("d", lo, hi)], [A_("ad", lo, hi)], W16)
+            o = (128 if least else 256) + CHW * k
+            out, E = T[P][:, o:o + CHW], ("ED" if least else "EZ")
+            l = [(out, T.ones[0:1, :], T.jrow[0:1, 0:CHW], True, False)] if least else []
+            for b in range(16):
+                l.append((out, T[E][:, 15 - b:143 - b], T.ad[:, a0:a1, 16 * b:16 * b + 16], b == 0 and not least, b == 15))
+            mms(l, [A_("ones"), A_("jrow"), A_(E), A_("ad", lo, hi)], [A_(P)])
+
+    def rotations(h):
+        w, RW = L128(h)
+        for q4 in range(4):
+            e = nextbank()
+            l, r = [], [RW("r16")]
+            for j in range(4):
+                c, rc = cmat(4 * q4 + j, 0)
+                r += rc
+                l.append((T[e][:, 128 * j:128 * j + 128], c, T.r16[:, w], True, True))
+            mms(l, r, [A_(e)], 128)
+            lo = 2048 * h + 512 * q4
+            actv(T.RTab[:, lo:lo + 512], T[e][:], ACT.Copy, [A_(e)], [A_("RTab", lo, lo + 512)], 512)
+
+    def least(t, h):
+        P = "P%d" % h
+        c8, R = T8(h)
+        w, RW = L128(h)
+        scan(T.km[:, w], T.rs[:], T[P][:, 128:256], 0.0, ALU.max, ALU.min, [A_("rs"), A_(P)], [RW("km")], 128)
+        tcopy(T.kk[:, c8], T.km[:, 128 * h + 15:128 * h + 128:16], [RW("km")], [R("kk")], 8)
+        if t < NRT:
+            ts(T.ks[:, c8], T.kk[:, c8], 15360, 3, ALU.bitwise_and, ALU.logical_shift_right, [R("kk")], [R("ks")])
+            tt(T.kq[:, c8], T.ks[:, c8], T.ili[:, 0:8], ALU.add, [R("ks"), A_("ili")], [R("kq")])
+            win, rw = T.RTab[:, 2048 * h:2048 * h + 2048], A_("RTab", 2048 * h, 2048 * h + 2048)
+        else:
+            ts(T.ks[:, c8], T.kk[:, c8], 15360, None, ALU.bitwise_and, None, [R("kk")], [R("ks")])
+            tt(T.kq[:, c8], T.ks[:, c8], T.cc[:, c8], ALU.add, [R("ks"), R("cc")], [R("kq")])
+            win, rw = T.RTR[:], A_("RTR")
+        tcopy(T.qo[:, c8], T.kq[:, c8], [R("kq")], [R("qo")], 8)
+        vgather(T.ql[:, w], win, T.qo[:, c8], [rw, R("qo")], [RW("ql")], 128)
+
+    def misc(lo, hi):
+        w, k = slice(lo, hi), hi - lo
+        RW = lambda b: A_(b, lo, hi)
+        tcopy(T.q16[:, w], T.ql[:, w], [RW("ql")], [RW("q16")], k // 2)
+        ts(T.n16[:, w], T.ql[:, w], 0.5, 1023.8, ALU.mult, ALU.add, [RW("ql")], [RW("n16")], k // 2)
+        mms([(T.L1[:, w], T.I4[:], T.n16[:, w], True, False), (T.L1[:, w], T.IM[:], T.q16[:, w], False, True)],
+            [A_("I4"), A_("IM"), RW("n16"), RW("q16")], [A_("L1")], k)
+        tt(T.zi[:, w], T.L0[:, w], T.q16[:, w], ALU.mult, [RW("q16"), A_("L0")], [RW("zi")], k)
+        ts(T.hi[:, w], T.zi[:, w], 5, 2047, ALU.logical_shift_right, ALU.bitwise_and, [RW("zi")], [RW("hi")], k)
+        ts(T.qc[:, w], T.L1[:, w], -4095.0, None, ALU.add, None, [A_("L1")], [RW("qc")], k)
+        tcopy(T.h16[:, w], T.hi[:, w], [RW("hi")], [RW("h16")], k)
+
+    def new_words(h, lens, rho):
+        e = nextbank()
+        w, RW = L128(h)
+        ls, r = [], []
+        for j, l in enumerate(lens):
+            if l < 10:
+                parts = [(l + 1, "w16")]
+            elif l == 16:
+                parts = [(0, "h16")]
+            else:
+                parts = [(MW + l - 10, "w16"), (MQ + l - 10, "qc"), (MH + l - 10, "h16")]
+            for k, (m, src) in enumerate(parts):
+                c, rc = cmat(m, rho)
+                r += rc + [RW(src)]
+                ls.append((T[e][:, 128 * j:128 * j + 128], c, T[src][:, w], k == 0, k == len(parts) - 1))
+        mms(ls, r, [A_(e)], 128)
+        lo, sz = 2176 * h + 128 * lens[0], 128 * len(lens)
+        actv(T.NT[:, lo:lo + sz], T[e][:, 0:sz], ACT.Copy, [A_(e)], [A_("NT", lo, lo + sz)], sz)
+
+    def match(h, rho):
+        P = "P%d" % h
+        c8, R = T8(h)
+        w, RW = L128(h)
+        tt(T.okb[:, w], T[P][:, 256:384], T.THe[:], ALU.is_le, [A_(P), A_("THe")], [RW("okb")], 128)
+        scan(T.hs[:, w], T.okb[:, w], T.ones[:], 1.0, ALU.mult, ALU.add, [RW("okb"), A_("ones")], [RW("hs")], 64)
+        ts(T.fm[:, c8], T.hs[:, 128 * h + 15:128 * h + 128:16], 17.0, 128.0, ALU.min, ALU.mult, [RW("hs")], [R("fm")])
+        c, rc = cmat(0, rho)
+        mms([(T[P][:, 384:392], c, T.fm[:, c8], True, False), (T[P][:, 384:392], T.IB[:], T.ilc[:, 0:8], False, True)],
+            rc + [A_("IB"), A_("ilc"), R("fm")], [A_(P)])
+        tcopy(T.fl[:, c8], T[P][:, 384:392], [A_(P)], [R("fl")], 8)
+
+    def send(t, h):
+        c8, R = T8(h)
+        w, RW = L128(h)
+        out, lo = ("S%d" % t if t < NV - 1 else "yf"), 2176 * h
+        vgather(T[out][:, w], T.NT[:, lo:lo + 2176], T.fl[:, c8], [A_("NT", lo, lo + 2176), R("fl")], [RW(out)], 128)
+        if t < NV - 1:
+            rid, pid = topo.addr(nxt, core)
+            dst, src, sem = T["W%d" % (t + 1)][:, w], T[out][:, w], T.sem["ar%d_%d" % (t + 1, h)]
+            op("g", [lambda: g.remote_dma(dst, src, sem, T.sem.ls, pid, rid, smask)], [RW(out)], [RW("W%d" % (t + 1))], 0.3, 2.6, "r")
+
+    def new_values(h):
+        lo = 2048 * h
+        w, RW = L128(h)
+        out = T.L1[:, 256 + 128 * h:384 + 128 * h]
+        mms([(out, T.IB[:], T.xw[:, lo + 15:lo + 2048:16], True, False), (out, T.IB[:], T.xw[:, lo:lo + 2048:16], False, False),
+             (out, T.IB[:], T.d[:, lo:lo + 2048:16], False, True)],
+            [A_("IB"), A_("xw", lo, lo + 2048), A_("d", lo, lo + 2048)], [A_("L1")], 128)
+        ts(T.nv[:, w], out, 0.5, -0.25, ALU.mult, ALU.add, [A_("L1")], [RW("nv")], 128)
+
+    def write_values():
+        ts(T.n2[:], T.hs[:, 15:256:16], 11.0, 2048.0, ALU.is_lt, ALU.mult, [A_("hs")], [A_("n2")])
+        tt(T.s2[:], T.n2[:], T.at[:], ALU.add, [A_("n2"), A_("at")], [A_("s2")])
+        tcopy(T.sl[:], T.s2[:], [A_("s2")], [A_("sl")], 16)
+        op("v", [lambda: vec.tensor_copy(T.xv[:].indirect(T.sl[:]), T.nv[:])], [A_("sl"), A_("nv")], [A_("xv")], 0.7)
+
+    def count():
+        ts(T.rp[:], T.hs[:, 15:256:16], 11.0, None, ALU.is_ge, None, [A_("hs")], [A_("rp")])
+        mms([(T.P0[:, 400:416], T.ones[:], T.rp[:], True, True)], [A_("ones"), A_("rp")], [A_("P0")])
+        actv(T.aj[:], T.P0[:, 400:416], ACT.Copy, [A_("P0")], [A_("aj"), A_("ac")], 16, accum_out=T.ac[:, 0:1])
+        tcopy(T.aci[:, 0:1], T.ac[:, 0:1], [A_("ac")], [A_("aci")], 1)
+        ts(T.acm[:, 0:1], T.aci[:, 0:1], 31, None, ALU.bitwise_and, None, [A_("aci")], [A_("acm")])
+        ts(T.a8[:, 0:1], T.acm[:, 0:1], 8.0, None, ALU.mult, None, [A_("acm")], [A_("a8")])
+        ts(T.THe[:], T.TH[:], T.a8[:, 0:1], None, ALU.add, None, [A_("TH"), A_("a8")], [A_("THe")], 128)
+
+    G = [[0, 1, 2, 3], [4, 5, 6, 7], [8, 9, 10, 11], [12, 13, 14, 15], [16]]
+    tcopy(T.THe[:], T.TH[:], [A_("TH")], [A_("THe")], 128)
+    for t in range(NV):
+        rho, W = GSH[t], "W%d" % t
+        for h in range(2):
+            w, RW = L128(h)
+            values(t, h)
+            u_sum(h)
+            expand(h)
+            relators(t, h)
+            tcopy(T.w16[:, w], T[W][:, w], [RW(W)], [RW("w16")], 64)
+            new_words(h, G[0], rho)
+            new_words(h, G[1], rho)
+            distances("rl", "X0", h, True)
+            if t < NRT:
+                rotations(h)
+        spread_u()
+        at_list()
+        for h in range(2):
+            least(t, h)
+            for lo, hi in MISC:
+                if hi == 128 * h + 128:
+                    misc(lo, hi)
+            distances("ql", "xw", h, False)
+            new_values(h)
+            if hi == 256 and len(MISC) == 1 and h == 0:
+                continue
+            for k in ((0, 1) if len(MISC) == 1 else (h,)):
+                for j in (2, 3, 4):
+                    new_words(k, G[j], rho)
+        for h in range(2):
+            match(h, rho)
+            send(t, h)
+        write_values()
+        if t < NV - 1:
+            count()
+
+    dma("y", T.yx[:], T.xv[:, 0:V], [A_("xv", 0, V)], [], "out0", 16, 5.0)
+    c, rc = cmat(REV, 0)
+    mms([(T.E0[:, 0:256], c, T.yf[:], True, True)], rc + [A_("yf")], [A_("E0")], 256)
+    tcopy(T.yo[:], T.E0[:, 0:256], [A_("E0")], [A_("yo")])
+    dma("s", T.yw[:], T.yo[:], [A_("yo")], [], "out1", 16, 3.0)
 
     Q = {"v": g.vector, "s": g.scalar, "t": g.tensor, "g": g, "y": g.sync}
-    cnt = {"v": 0, "s": 0, "t": 0, "g": 0}
+    cnt = {q: 0 for q in Q}
     seen = {q: {} for q in Q}
-    snap = {}
-    acc = {}
+    snap, acc = {}, {}
 
     def need(q, tok):
         s, val = tok
@@ -95,511 +507,58 @@ def rank_program(g, core, T, topo):
 
     def deps(q, reads, writes):
         toks = {}
-        for (regs, wr) in ((reads, False), (writes, True)):
-            for (b, lo, hi) in regs:
-                for (l2, h2, q2, tok, w2) in acc.get(b, []):
+        for regs, wr in ((reads, False), (writes, True)):
+            for b, lo, hi in regs:
+                for l2, h2, q2, tok, w2 in acc.get(b, ()):
                     if b in PSUM:
                         if q2 == q:
                             continue
-                    else:
-                        if l2 >= hi or h2 <= lo or not (wr or w2):
-                            continue
-                        if q2 == q and (wr or not w2):
-                            continue
+                    elif l2 >= hi or h2 <= lo or not (wr or w2):
+                        continue
                     toks[tok[0]] = max(toks.get(tok[0], 0), tok[1])
         for s in sorted(toks):
             need(q, (s, toks[s]))
 
     def note(q, reads, writes, tok):
-        snap[tok] = dict(seen[q])
-        for (b, lo, hi) in writes:
-            old = acc.get(b, [])
-            if b in PSUM:
-                acc[b] = [e for e in old if e[2] != q and e[4] and False] + [[lo, hi, q, tok, True]]
-            else:
-                acc[b] = [e for e in old if not (e[0] >= lo and e[1] <= hi)] + [[lo, hi, q, tok, True]]
-        for (b, lo, hi) in reads:
-            if b in PSUM:
-                acc[b] = [[lo, hi, q, tok, True]]
-            else:
-                acc[b] = [e for e in acc.get(b, []) if not (e[2] == q and not e[4] and e[0] >= lo and e[1] <= hi)] + [[lo, hi, q, tok, False]]
-
-    def op(q, fn, reads, writes):
-        deps(q, reads, writes)
-        cnt[q] += 1
-        s = "q" + q
-        fn().then_inc(T.sem[s], 1)
-        note(q, reads, writes, (s, cnt[q]))
-
-    def dma(q, out, in_, reads, writes, sem, total):
-        deps(q, reads, writes)
-        Q[q].dma_start(out, in_).then_inc(T.sem[sem], 16)
-        note("dma_" + sem, reads, writes, (sem, total)) if False else None
-        snap[(sem, total)] = dict(seen[q])
-        for (b, lo, hi) in writes:
-            acc.setdefault(b, []).append([lo, hi, "dma", (sem, total), True])
-        for (b, lo, hi) in reads:
-            acc.setdefault(b, []).append([lo, hi, "dma", (sem, total), False])
-
-    A_ = lambda b, lo=0, hi=1 << 20: (b, lo, hi)
-    vec, sca, ten = g.vector, g.scalar, g.tensor
-
-    def tcopy(out, in_, r, w):
-        op("v", lambda: vec.tensor_copy(out, in_), r, w)
-
-    def tt(out, a, b, o, r, w):
-        op("v", lambda: vec.tensor_tensor(out, a, b, o), r, w)
-
-    def ts(out, a, s1, s2, o0, o1, r, w):
-        if o1 is None:
-            op("v", lambda: vec.tensor_scalar(out, a, s1, None, o0), r, w)
-        else:
-            op("v", lambda: vec.tensor_scalar(out, a, s1, s2, o0, o1), r, w)
-
-    def mset(ap, c, w):
-        op("v", lambda: vec.memset(ap, c), [], w)
-
-    def actv(out, in_, f, r, w, **kw):
-        op("s", lambda: sca.activation(out, in_, f, **kw), r, w)
-
-    def mm(out, l, r_, st, sp, r, w):
-        op("t", lambda: ten.matmul(out, l, r_, st, sp), r, w)
-
-    def iota(out, pat, base, cm, w):
-        op("g", lambda: g.iota(out, pat, base, cm), [], w)
-
-    dma("s", T.wdi[:], T.wd[:], [], [A_("wdi")], "ld0", 16)
-    dma("y", T.xv[:, 0:V], T.x[:], [], [A_("xv")], "ld1", 16)
-    dma("s", T.rti[:, 712:1024], T.rt[:, 0:312], [], [A_("rti", 712, 1024)], "ld2", 16)
-    dma("s", T.rti[:, 0:712], T.rt[:, 312:1024], [], [A_("rti", 0, 712)], "ld3", 16)
-    dma("y", T.wti[:, 0:1], T.wt[:], [], [A_("wti")], "ld4", 16)
-    dma("y", T.thi[:, 0:1], T.th[:], [], [A_("thi")], "ld5", 16)
-
-    iota(T.pc[:, 0:1], [[1, 1]], 0, 1, [A_("pc")])
-    iota(T.row[:, 0:144], [[1, 144]], 0, 0, [A_("row")])
-    iota(T.grow[:], [[1, 8], [0, 16]], 0, 0, [A_("grow")])
-    iota(T.krow[:], [[0, 8], [1, 16]], 0, 0, [A_("krow")])
-    iota(T.gam[:, 0:10], [[1, 10]], 6, 0, [A_("gam")])
-    iota(T.ai[:], [[16, 16]], 0, 0, [A_("ai")])
-    iota(T.tga[:], [[-1, 16], [1, 16]], 16, 0, [A_("tga")])
-    mset(T.tgt[:, 256:560], -1, [A_("tgt", 256, 560)])
-    iota(T.tgt[:, REV * 16:REV * 16 + 16], [[-1, 16]], 15, 0, [A_("tgt", REV * 16, REV * 16 + 16)])
-    for l in range(10, 16):
-        a = (MQ + l - 10) * 16
-        iota(T.tgt[:, a + l:a + 16], [[-1, 16 - l]], 15 - l, 0, [A_("tgt", a + l, a + 16)])
-        a = (MW + l - 10) * 16
-        iota(T.tgt[:, a + 2 * l - 16:a + l], [[1, 16 - l]], 0, 0, [A_("tgt", a + 2 * l - 16, a + l)])
-        a = (MH + l - 10) * 16
-        iota(T.tgt[:, a:a + 2 * l - 16], [[1, 2 * l - 16]], 0, 0, [A_("tgt", a, a + 2 * l - 16)])
-
-    ts(T.ki[:, 0:1], T.pc[:, 0:1], 15, None, ALU.bitwise_and, None, [A_("pc")], [A_("ki")])
-    ts(T.gi[:, 0:1], T.pc[:, 0:1], 4, None, ALU.logical_shift_right, None, [A_("pc")], [A_("gi")])
-    tcopy(T.pf[:, 0:1], T.pc[:, 0:1], [A_("pc")], [A_("pf")])
-    tcopy(T.kf[:, 0:1], T.ki[:, 0:1], [A_("ki")], [A_("kf")])
-    tcopy(T.gf[:, 0:1], T.gi[:, 0:1], [A_("gi")], [A_("gf")])
-    ts(T.g16[:, 0:1], T.gf[:, 0:1], 16.0, 15.0, ALU.mult, ALU.add, [A_("gf")], [A_("g16")])
-    ts(T.kr15[:, 0:1], T.kf[:, 0:1], -1.0, 15.0, ALU.mult, ALU.add, [A_("kf")], [A_("kr15")])
-    ts(T.tgt[:, 0:256], T.tga[:], 15, None, ALU.bitwise_and, None, [A_("tga")], [A_("tgt", 0, 256)])
-    ts(T.gam[:, 0:10], T.gam[:, 0:10], 7, None, ALU.bitwise_and, None, [A_("gam")], [A_("gam")])
-    ts(T.bm[:, 0:10], T.gam[:, 0:10], T.gf[:, 0:1], None, ALU.is_equal, None, [A_("gam"), A_("gf")], [A_("bm")])
-    for m in range(NM):
-        pass
-    op("v", lambda: vec.tensor_scalar(T.F1[:], T.tgt[:], T.kf[:, 0:1], None, ALU.is_equal),
-       [A_("tgt"), A_("kf")], [A_("F1")])
-    for j in range(10):
-        o = T.CM[:, :, 16 * j:16 * j + 16]
-        sc = T.bm[:, j:j + 1]
-        if j % 2 == 0:
-            ts(o, T.F1[:], sc, None, ALU.mult, None, [A_("F1"), A_("bm")], [A_("CM", j, j + 1)])
-        else:
-            actv(o, T.F1[:], ACT.Copy, [A_("F1"), A_("bm")], [A_("CM", j, j + 1)], scale=sc)
-
-    def cmat(m, rho):
-        lo = 16 * (2 - rho)
-        return T.CM[:, m, lo:lo + 128], A_("CM", 2 - rho, 10 - rho)
-
-    tcopy(T.wd16[:], T.wdi[:], [A_("wdi")], [A_("wd16")])
-    c, rc = cmat(REV, 0)
-    mm(T.E0[:, 0:256], c, T.wd16[:], True, True, [rc, A_("wd16")], [A_("E0")])
-    tcopy(T.W0[:], T.E0[:, 0:256], [A_("E0")], [A_("W0")])
-    tcopy(T.rt16[:], T.rti[:], [A_("rti")], [A_("rt16")])
-    for k in range(2):
-        e = "E%d" % (1 + k)
-        mm(T[e][:], c, T.rt16[:, 512 * k:512 * k + 512], True, True, [rc, A_("rt16")], [A_(e)])
-        actv(T.RT0[:, 512 * k:512 * k + 512], T[e][:], ACT.Copy, [A_(e)], [A_("RT0", 512 * k, 512 * k + 512)])
-    dma("y", T.RD[:, 0:16, :], T.RT0[:], [A_("RT0")], [A_("RD")], "rd", 32)
-    dma("y", T.RD[:, 16:32, :], T.RT0[:], [A_("RT0")], [], "rd", 32)
-    for s in range(16):
-        dma("y", T.RTR[:, 1024 * s:1024 * s + 1024], T.RD[:, 16 - s:32 - s, :], [A_("RD")], [A_("RTR")] if s == 0 else [], "rtl", 256)
-
-    ts(T.wlo_i[:, 0:1], T.wti[:, 0:1], 255, None, ALU.bitwise_and, None, [A_("wti")], [A_("wlo_i")])
-    ts(T.whi_i[:, 0:1], T.wti[:, 0:1], 3840, None, ALU.bitwise_and, None, [A_("wti")], [A_("whi_i")])
-    tcopy(T.wlo[:, 0:1], T.wlo_i[:, 0:1], [A_("wlo_i")], [A_("wlo")])
-    tcopy(T.whi[:, 0:1], T.whi_i[:, 0:1], [A_("whi_i")], [A_("whi")])
-    sel = [A_("row"), A_("g16")]
-    ts(T.WZh[:], T.row[:], T.g16[:, 0:1], T.whi[:, 0:1], ALU.is_equal, ALU.mult, sel + [A_("whi")], [A_("WZh")])
-    ts(T.WZl[:], T.row[:], T.g16[:, 0:1], T.wlo[:, 0:1], ALU.is_equal, ALU.mult, sel + [A_("wlo")], [A_("WZl")])
-    ts(T.ED[:], T.row[:], T.g16[:, 0:1], 16384.0, ALU.is_equal, ALU.mult, sel, [A_("ED")])
-    ts(T.EZ[:], T.row[:], T.g16[:, 0:1], None, ALU.is_equal, None, sel, [A_("EZ")])
-    ts(T.WBh[:], T.grow[:], T.gf[:, 0:1], T.whi[:, 0:1], ALU.is_equal, ALU.mult, [A_("grow"), A_("gf"), A_("whi")], [A_("WBh")])
-    ts(T.WBl[:], T.grow[:], T.gf[:, 0:1], T.wlo[:, 0:1], ALU.is_equal, ALU.mult, [A_("grow"), A_("gf"), A_("wlo")], [A_("WBl")])
-    mset(T.Z[:], 0.0, [A_("Z")])
-    mset(T.hold[:], 1.0, [A_("hold")])
-    op("v", lambda: vec.memset(T.hold[:, 0:2048:16], 0.0), [A_("hold")], [A_("hold")])
-    mset(T.ones[:], 1.0, [A_("ones")])
-    ts(T.jrow[:], T.krow[:, 0:64], -1024.0, 15360.0, ALU.mult, ALU.add, [A_("krow")], [A_("jrow")])
-    ts(T.rs[:], T.krow[:], 0.0, 1e9, ALU.is_equal, ALU.mult, [A_("krow")], [A_("rs")])
-    ts(T.ilf[:], T.ai[:], T.kf[:, 0:1], None, ALU.add, None, [A_("ai"), A_("kf")], [A_("ilf")])
-    tcopy(T.ili[:], T.ilf[:], [A_("ilf")], [A_("ili")])
-    ts(T.i8[:], T.ilf[:], 8.0, None, ALU.mult, None, [A_("ilf")], [A_("i8")])
-    ts(T.dm[:], T.ilf[:], 2048.0, None, ALU.add, None, [A_("ilf")], [A_("dm")])
-    irow = T.row[:, 0:128]
-    ts(T.IB[:], irow, T.pf[:, 0:1], None, ALU.is_equal, None, [A_("row"), A_("pf")], [A_("IB")])
-
-    def late_constants():
-        ts(T.ilc[:, 0:8], T.ilf[:, 0:8], -128.0, None, ALU.add, None, [A_("ilf")], [A_("ilc")])
-        ts(T.I4[:], irow, T.pf[:, 0:1], 4.0, ALU.is_equal, ALU.mult, [A_("row"), A_("pf")], [A_("I4")])
-        ts(T.IM[:], irow, T.pf[:, 0:1], -1.0, ALU.is_equal, ALU.mult, [A_("row"), A_("pf")], [A_("IM")])
-        tcopy(T.thf[:, 0:1], T.thi[:, 0:1], [A_("thi")], [A_("thf")])
-        ts(T.BO[:], T.grow[:], T.gf[:, 0:1], None, ALU.is_equal, None, [A_("grow"), A_("gf")], [A_("BO")])
-        ts(T.thr[:], T.krow[:], T.kr15[:, 0:1], T.thf[:, 0:1], ALU.is_equal, ALU.mult, [A_("krow"), A_("kr15"), A_("thf")], [A_("thr")])
-        mm(T.L1[:, 384:512], T.BO[:], T.thr[:], True, True, [A_("BO"), A_("thr")], [A_("L1")])
-        tcopy(T.TH[:], T.L1[:, 384:512], [A_("L1")], [A_("TH")])
-        for r in (1, 2):
-            src = T.CM[:, 0, 16 * (2 - r):16 * (2 - r) + 128]
-            tcopy(T.rot[:, r, :], src, [A_("CM")], [A_("rot", r, r + 1)])
-
-    ebank = [0]
-
-    def nextbank():
-        ebank[0] = (ebank[0] + 1) % 4
-        return "E%d" % ebank[0]
-
-    def gather_values(q, t, lo, hi):
-        w = "W%d" % t
-        src = T.xv[:, 0:V].indirect(T[w][:, lo:hi])
-        out = T.xw[:, 16 * lo:16 * hi]
-        r = [A_("xv"), A_(w, lo, hi)]
-        if q == "v":
-            tcopy(out, src, r, [A_("xw", 16 * lo, 16 * hi)])
-        else:
-            actv(out, src, ACT.Copy, r, [A_("xw", 16 * lo, 16 * hi)])
-
-    def pe_u(h):
-        P, L, lo = "P%d" % h, "L%d" % h, 2048 * h
-        rx = A_("xw", lo, lo + 2048)
-        for b in range(16):
-            rhs = T.xw[:, lo + 16 * b + 15:lo + 2048:256]
-            mm(T[P][:, 0:8], T.WZh[:, 15 - b:143 - b], rhs, b == 0, False, [rx, A_("WZh")], [A_(P)])
-            mm(T[P][:, 0:8], T.WZl[:, 15 - b:143 - b], rhs, False, b == 15, [rx, A_("WZl")], [A_(P)])
-        rhs = T.xw[:, lo + 15:lo + 2048:16]
-        mm(T[L][:, 0:128], T.WBh[:], rhs, True, False, [rx, A_("WBh")], [A_(L)])
-        mm(T[L][:, 0:128], T.WBl[:], rhs, False, True, [rx, A_("WBl")], [A_(L)])
-
-    def expand(h):
-        lo = 2048 * h
-        R = lambda b: A_(b, lo, lo + 2048)
-        tcopy(T.Z[:, lo:lo + 2048:16], T.xw[:, lo + 15:lo + 2048:16], [R("xw")], [R("Z")])
-        op("v", lambda: vec.tensor_tensor_scan(T.X0[:, lo:lo + 2048], T.hold[:], T.Z[:, lo:lo + 2048], 0.0, ALU.mult, ALU.add),
-           [A_("hold"), R("Z")], [R("X0")])
-
-    def relators(t, h):
-        P = "P%d" % h
-        c8 = slice(8 * h, 8 * h + 8)
-        R = lambda b: A_(b, 8 * h, 8 * h + 8)
-        tcopy(T.ui[:, c8], T[P][:, 0:8], [A_(P)], [R("ui")])
-        ts(T.uu[:, c8], T.ui[:, c8], 4095, None, ALU.bitwise_and, None, [R("ui")], [R("uu")])
-        ts(T.tf[:, c8], T.uu[:, c8], 592.0, None, ALU.add, None, [R("uu")], [R("tf")])
-        tt(T.zz[:, c8], T.tf[:, c8], T.tf[:, c8], ALU.mult, [R("tf")], [R("zz")])
-        ts(T.cc[:, c8], T.zz[:, c8], 5, 1023, ALU.logical_shift_right, ALU.bitwise_and, [R("zz")], [R("cc")])
-        tcopy(T.cl[:, c8], T.cc[:, c8], [R("cc")], [R("cl")])
-        w = slice(128 * h, 128 * h + 128)
-        RW = lambda b: A_(b, 128 * h, 128 * h + 128)
-        tcopy(T.rl[:, w], T.RT0[:].indirect(T.cl[:, c8]), [A_("RT0"), R("cl")], [RW("rl")])
-        if t < NRT:
-            tcopy(T.r16[:, w], T.rl[:, w], [RW("rl")], [RW("r16")])
-
-    def at_list(h):
-        c8 = slice(8 * h, 8 * h + 8)
-        R = lambda b: A_(b, 8 * h, 8 * h + 8)
-        ts(T.u7[:, c8], T.ui[:, c8], 7, None, ALU.bitwise_and, None, [R("ui")], [R("u7")])
-        tt(T.at[:, c8], T.u7[:, c8], T.i8[:, c8], ALU.add, [R("u7"), A_("i8")], [R("at")])
-
-    def sub(lst, other, ch):
-        lo, w0 = 1024 * ch, 64 * ch
-        op("v", lambda: vec.tensor_tensor(T.d[:, lo:lo + 1024], T.xv[:, 0:V].indirect(T[lst][:, w0:w0 + 64]), T[other][:, lo:lo + 1024], ALU.subtract),
-           [A_("xv"), A_(lst, w0, w0 + 64), A_(other, lo, lo + 1024)], [A_("d", lo, lo + 1024)])
-
-    def size(ch):
-        lo = 1024 * ch
-        actv(T.ad[:, 4 * ch:4 * ch + 4, :], T.d[:, lo:lo + 1024], ACT.Abs, [A_("d", lo, lo + 1024)], [A_("ad", lo, lo + 1024)])
-
-    def pe_sum(ch, least):
-        P, k = "P%d" % (ch // 2), ch % 2
-        o = (128 if least else 256) + 64 * k
-        out = T[P][:, o:o + 64]
-        E = "ED" if least else "EZ"
-        if least:
-            mm(out, T.ones[0:1, :], T.jrow[0:1, :], True, False, [A_("ones"), A_("jrow")], [A_(P)])
-        for b in range(16):
-            mm(out, T[E][:, 15 - b:143 - b], T.ad[:, 4 * ch:4 * ch + 4, 16 * b:16 * b + 16], b == 0 and not least, b == 15,
-               [A_(E), A_("ad", 1024 * ch, 1024 * ch + 1024)], [A_(P)])
-
-    def pe_rtab(h):
-        RW = A_("r16", 128 * h, 128 * h + 128)
-        for q4 in range(4):
-            e = nextbank()
-            for j in range(4):
-                c, rc = cmat(4 * q4 + j, 0)
-                mm(T[e][:, 128 * j:128 * j + 128], c, T.r16[:, 128 * h:128 * h + 128], True, True, [rc, RW], [A_(e)])
-            lo = 2048 * h + 512 * q4
-            actv(T.RTab[:, lo:lo + 512], T[e][:], ACT.Copy, [A_(e)], [A_("RTab", lo, lo + 512)])
-
-    def least(t, h):
-        P = "P%d" % h
-        c8, w = slice(8 * h, 8 * h + 8), slice(128 * h, 128 * h + 128)
-        R = lambda b: A_(b, 8 * h, 8 * h + 8)
-        RW = lambda b: A_(b, 128 * h, 128 * h + 128)
-        op("v", lambda: vec.tensor_tensor_scan(T.km[:, w], T.rs[:], T[P][:, 128:256], 0.0, ALU.max, ALU.min), [A_("rs"), A_(P)], [RW("km")])
-        tcopy(T.kk[:, c8], T.km[:, 128 * h + 15:128 * h + 128:16], [RW("km")], [R("kk")])
-        if t < NRT:
-            ts(T.ks[:, c8], T.kk[:, c8], 15360, 3, ALU.bitwise_and, ALU.logical_shift_right, [R("kk")], [R("ks")])
-            tt(T.kq[:, c8], T.ks[:, c8], T.ili[:, 0:8], ALU.add, [R("ks"), A_("ili")], [R("kq")])
-            win, rw = T.RTab[:, 2048 * h:2048 * h + 2048], A_("RTab", 2048 * h, 2048 * h + 2048)
-        else:
-            ts(T.ks[:, c8], T.kk[:, c8], 15360, None, ALU.bitwise_and, None, [R("kk")], [R("ks")])
-            tt(T.kq[:, c8], T.ks[:, c8], T.cc[:, c8], ALU.add, [R("ks"), R("cc")], [R("kq")])
-            win, rw = T.RTR[:], A_("RTR")
-        tcopy(T.qo[:, c8], T.kq[:, c8], [R("kq")], [R("qo")])
-        tcopy(T.ql[:, w], win.indirect(T.qo[:, c8]), [rw, R("qo")], [RW("ql")])
-
-    def misc(h):
-        L = "L%d" % h
-        w = slice(128 * h, 128 * h + 128)
-        RW = lambda b: A_(b, 128 * h, 128 * h + 128)
-        tcopy(T.q16[:, w], T.ql[:, w], [RW("ql")], [RW("q16")])
-        ts(T.n16[:, w], T.ql[:, w], 0.5, 1023.8, ALU.mult, ALU.add, [RW("ql")], [RW("n16")])
-        mm(T[L][:, 128:256], T.I4[:], T.n16[:, w], True, False, [A_("I4"), RW("n16")], [A_(L)])
-        mm(T[L][:, 128:256], T.IM[:], T.q16[:, w], False, True, [A_("IM"), RW("q16")], [A_(L)])
-        tcopy(T.uli[:, w], T[L][:, 0:128], [A_(L)], [RW("uli")])
-        ts(T.ulm[:, w], T.uli[:, w], 4095, None, ALU.bitwise_and, None, [RW("uli")], [RW("ulm")])
-        ts(T.ul[:, w], T.ulm[:, w], 32.0, None, ALU.add, None, [RW("ulm")], [RW("ul")])
-        tt(T.zi[:, w], T.q16[:, w], T.ul[:, w], ALU.mult, [RW("q16"), RW("ul")], [RW("zi")])
-        ts(T.hi[:, w], T.zi[:, w], 5, 2047, ALU.logical_shift_right, ALU.bitwise_and, [RW("zi")], [RW("hi")])
-        tcopy(T.h16[:, w], T.hi[:, w], [RW("hi")], [RW("h16")])
-        ts(T.qc[:, w], T[L][:, 128:256], -4095.0, None, ALU.add, None, [A_(L)], [RW("qc")])
-
-    def pe_new(h, lens, rho):
-        e = nextbank()
-        w = slice(128 * h, 128 * h + 128)
-        RW = lambda b: A_(b, 128 * h, 128 * h + 128)
-        for j, l in enumerate(lens):
-            if l < 10:
-                parts = [(l + 1, "w16")]
-            elif l == 16:
-                parts = [(0, "h16")]
-            else:
-                parts = [(MW + l - 10, "w16"), (MQ + l - 10, "qc"), (MH + l - 10, "h16")]
-            for k, (m, src) in enumerate(parts):
-                c, rc = cmat(m, rho)
-                mm(T[e][:, 128 * j:128 * j + 128], c, T[src][:, w], k == 0, k == len(parts) - 1, [rc, RW(src)], [A_(e)])
-        return e
-
-    def evac(h, lens, e):
-        lo, sz = 2176 * h + 128 * lens[0], 128 * len(lens)
-        actv(T.NT[:, lo:lo + sz], T[e][:, 0:sz], ACT.Copy, [A_(e)], [A_("NT", lo, lo + sz)])
-
-    def match(h):
-        P = "P%d" % h
-        c8, w = slice(8 * h, 8 * h + 8), slice(128 * h, 128 * h + 128)
-        R = lambda b: A_(b, 8 * h, 8 * h + 8)
-        RW = lambda b: A_(b, 128 * h, 128 * h + 128)
-        tt(T.okb[:, w], T[P][:, 256:384], T.THe[:], ALU.is_le, [A_(P), A_("THe")], [RW("okb")])
-        op("v", lambda: vec.tensor_tensor_scan(T.hs[:, w], T.okb[:, w], T.ones[:], 1.0, ALU.mult, ALU.add),
-           [RW("okb"), A_("ones")], [RW("hs")])
-        ts(T.fm[:, c8], T.hs[:, 128 * h + 15:128 * h + 128:16], 17.0, 128.0, ALU.min, ALU.mult, [RW("hs")], [R("fm")])
-        tt(T.fo[:, c8], T.fm[:, c8], T.ilc[:, 0:8], ALU.add, [R("fm"), A_("ilc")], [R("fo")])
-
-    def pe_list(h, rho):
-        P = "P%d" % h
-        mm(T[P][:, 384:392], T.rot[:, rho, :], T.fo[:, 8 * h:8 * h + 8], True, True, [A_("rot", rho, rho + 1), A_("fo", 8 * h, 8 * h + 8)], [A_(P)])
-
-    def final(t, h):
-        c8, w = slice(8 * h, 8 * h + 8), slice(128 * h, 128 * h + 128)
-        R = lambda b: A_(b, 8 * h, 8 * h + 8)
-        P = "P%d" % h
-        rho = GSH[t]
-        if rho:
-            pe_list(h, rho)
-
-    def final2(t, h):
-        c8, w = slice(8 * h, 8 * h + 8), slice(128 * h, 128 * h + 128)
-        R = lambda b: A_(b, 8 * h, 8 * h + 8)
-        P = "P%d" % h
-        if GSH[t]:
-            tcopy(T.fl[:, c8], T[P][:, 384:392], [A_(P)], [R("fl")])
-        else:
-            tcopy(T.fl[:, c8], T.fo[:, c8], [R("fo")], [R("fl")])
-        out = "S%d" % t if t < NV - 1 else "yf"
-        lo = 2176 * h
-        tcopy(T[out][:, w], T.NT[:, lo:lo + 2176].indirect(T.fl[:, c8]), [A_("NT", lo, lo + 2176), R("fl")], [A_(out, 128 * h, 128 * h + 128)])
-        if t < NV - 1:
-            deps("g", [A_(out, 128 * h, 128 * h + 128)], [])
-            rid, pid = topo.addr(nxt, core)
-            g.remote_dma(T["W%d" % (t + 1)][:, w], T[out][:, w], T.sem["ar%d_%d" % (t + 1, h)], T.sem.ls, pid, rid, smask)
-
-    def eng_mask(src, dst):
-        return sum(1 << e for e in topo.engines(src, dst)[:8])
-
-    smask = eng_mask(core, nxt)
-    n_in = len(topo.engines(prv, core)[:8])
-    n_out = len(topo.engines(core, nxt)[:8])
-
-    def pe_nv(h):
-        L, lo = "L%d" % h, 2048 * h
-        rx, rd = A_("xw", lo, lo + 2048), A_("d", lo, lo + 2048)
-        out = T[L][:, 256:384]
-        mm(out, T.IB[:], T.xw[:, lo + 15:lo + 2048:16], True, False, [rx, A_("IB")], [A_(L)])
-        mm(out, T.IB[:], T.xw[:, lo:lo + 2048:16], False, False, [rx, A_("IB")], [A_(L)])
-        mm(out, T.IB[:], T.d[:, lo:lo + 2048:16], False, True, [rd, A_("IB")], [A_(L)])
-
-    def new_values(h):
-        L, w = "L%d" % h, slice(128 * h, 128 * h + 128)
-        ts(T.nv[:, w], T[L][:, 256:384], 0.5, -0.25, ALU.mult, ALU.add, [A_(L)], [A_("nv", 128 * h, 128 * h + 128)])
-
-    def write_list(h):
-        c8 = slice(8 * h, 8 * h + 8)
-        R = lambda b: A_(b, 8 * h, 8 * h + 8)
-        ts(T.yb[:, c8], T.fo[:, c8], -8192.0, 10481664.0, ALU.mult, ALU.add, [R("fo")], [R("yb")])
-        tt(T.s1[:, c8], T.yb[:, c8], T.dm[:, c8], ALU.min, [R("yb"), A_("dm")], [R("s1")])
-        tt(T.s2[:, c8], T.s1[:, c8], T.at[:, c8], ALU.max, [R("s1"), R("at")], [R("s2")])
-        tcopy(T.sl[:, c8], T.s2[:, c8], [R("s2")], [R("sl")])
-
-    def scatter():
-        tcopy(T.xv[:].indirect(T.sl[:]), T.nv[:], [A_("sl"), A_("nv")], [A_("xv")])
-
-    def count():
-        for h in range(2):
-            c8 = slice(8 * h, 8 * h + 8)
-            ts(T.rp[:, c8], T.fo[:, c8], 1280.0, None, ALU.is_ge, None, [A_("fo", 8 * h, 8 * h + 8)], [A_("rp", 8 * h, 8 * h + 8)])
-        mm(T.P0[:, 400:416], T.ones[:], T.rp[:], True, True, [A_("ones"), A_("rp")], [A_("P0")])
-        actv(T.aj[:], T.P0[:, 400:416], ACT.Copy, [A_("P0")], [A_("aj"), A_("ac")], accum_out=T.ac[:, 0:1])
-
-    def allowance():
-        tcopy(T.aci[:, 0:1], T.ac[:, 0:1], [A_("ac")], [A_("aci")])
-        ts(T.acm[:, 0:1], T.aci[:, 0:1], 31, None, ALU.bitwise_and, None, [A_("aci")], [A_("acm")])
-        ts(T.a8[:, 0:1], T.acm[:, 0:1], 8.0, None, ALU.mult, None, [A_("acm")], [A_("a8")])
-        ts(T.THe[:], T.TH[:], T.a8[:, 0:1], None, ALU.add, None, [A_("TH"), A_("a8")], [A_("THe")])
+        snap[tok] = dict(seen[q if q in seen else "g"]) if q in seen else {}
+        for regs, wr in ((reads, False), (writes, True)):
+            for b, lo, hi in regs:
+                old = acc.get(b, [])
+                if b in PSUM:
+                    acc[b] = [[lo, hi, q, tok, True]]
+                elif wr:
+                    acc[b] = [e for e in old if not (e[0] >= lo and e[1] <= hi)] + [[lo, hi, q, tok, True]]
+                else:
+                    acc[b] = [e for e in old if not (e[2] == q and not e[4] and e[0] >= lo and e[1] <= hi)] + [[lo, hi, q, tok, False]]
 
     for t in range(1, NV):
         for h in range(2):
             acc.setdefault("W%d" % t, []).append([128 * h, 128 * h + 128, "remote", ("ar%d_%d" % (t, h), n_in), True])
-
-    for t in range(NV):
-        rho = GSH[t]
-        G = [[0, 1, 2, 3], [4, 5, 6, 7], [8, 9, 10, 11], [12, 13, 14, 15], [16]]
-        W = "W%d" % t
-        gather_values("s", t, 0, 64)
-        gather_values("v", t, 64, 128)
-        pe_u(0)
-        gather_values("s", t, 128, 256)
-        expand(0)
-        tcopy(T.w16[:, 0:128], T[W][:, 0:128], [A_(W, 0, 128)], [A_("w16", 0, 128)])
-        relators(t, 0)
-        turned = {}
-        turned[(0, 0)] = pe_new(0, G[0], rho)
-        turned[(0, 1)] = pe_new(0, G[1], rho)
-        pe_u(1)
-        sub("rl", "X0", 0)
-        evac(0, G[0], turned[(0, 0)])
-        size(0)
-        sub("rl", "X0", 1)
-        evac(0, G[1], turned[(0, 1)])
-        size(1)
-        tcopy(T.w16[:, 128:256], T[W][:, 128:256], [A_(W, 128, 256)], [A_("w16", 128, 256)])
-        expand(1)
-        relators(t, 1)
-        pe_sum(0, True)
-        pe_sum(1, True)
-        if t < NRT:
-            pe_rtab(0)
-        turned[(1, 0)] = pe_new(1, G[0], rho)
-        turned[(1, 1)] = pe_new(1, G[1], rho)
-        sub("rl", "X0", 2)
-        evac(1, G[0], turned[(1, 0)])
-        size(2)
-        if t == 0:
-            late_constants()
-            tcopy(T.THe[:], T.TH[:], [A_("TH")], [A_("THe")])
+    for i in schedule(ops):
+        o = ops[i]
+        q = o["q"]
+        if o["kind"] == "r":
+            deps(q, o["r"], [])
+            o["f"][0]()
+        elif o["kind"] == "d":
+            deps(q, o["r"], o["w"])
+            sem, total = o["sem"]
+            o["f"][0]().then_inc(T.sem[sem], 16)
+            before = dict(seen[q])
+            note("dma", o["r"], o["w"], (sem, total))
+            snap[(sem, total)] = before
         else:
-            allowance()
-        least(t, 0)
-        sub("rl", "X0", 3)
-        evac(1, G[1], turned[(1, 1)])
-        size(3)
-        pe_sum(2, True)
-        pe_sum(3, True)
-        if t < NRT:
-            pe_rtab(1)
-        sub("ql", "xw", 0)
-        size(0)
-        at_list(0)
-        at_list(1)
-        misc(0)
-        sub("ql", "xw", 1)
-        size(1)
-        pe_sum(0, False)
-        pe_sum(1, False)
-        pe_nv(0)
-        e2 = pe_new(0, G[2], rho)
-        e3 = pe_new(0, G[3], rho)
-        e4 = pe_new(0, G[4], rho)
-        least(t, 1)
-        sub("ql", "xw", 2)
-        evac(0, G[2], e2)
-        evac(0, G[3], e3)
-        size(2)
-        evac(0, G[4], e4)
-        misc(1)
-        sub("ql", "xw", 3)
-        size(3)
-        pe_sum(2, False)
-        f2 = pe_new(1, G[2], rho)
-        pe_sum(3, False)
-        pe_nv(1)
-        f3 = pe_new(1, G[3], rho)
-        f4 = pe_new(1, G[4], rho)
-        evac(1, G[2], f2)
-        evac(1, G[3], f3)
-        evac(1, G[4], f4)
-        match(0)
-        final(t, 0)
-        new_values(0)
-        write_list(0)
-        final2(t, 0)
-        match(1)
-        final(t, 1)
-        new_values(1)
-        write_list(1)
-        scatter()
-        final2(t, 1)
-        if t < NV - 1:
-            count()
-
-    dma("y", T.yx[:], T.xv[:, 0:V], [A_("xv")], [], "out0", 16)
-    c, rc = cmat(REV, 0)
-    mm(T.E0[:, 0:256], c, T.yf[:], True, True, [rc, A_("yf")], [A_("E0")])
-    tcopy(T.yo[:], T.E0[:, 0:256], [A_("E0")], [A_("yo")])
-    dma("s", T.yw[:], T.yo[:], [A_("yo")], [], "out1", 16)
+            deps(q, o["r"], o["w"])
+            for f in o["f"]:
+                cnt[q] += 1
+                f().then_inc(T.sem["q" + q], 1)
+            note(q, o["r"], o["w"], ("q" + q, cnt[q]))
     for q in ("v", "s", "t", "g"):
         need("g", ("q" + q, cnt[q]))
     for k in range(6):
         need("g", ("ld%d" % k, 16))
-    need("g", ("rd", 32))
-    need("g", ("rtl", 256))
     for t in range(1, NV):
         for h in range(2):
             need("g", ("ar%d_%d" % (t, h), n_in))
-    need("g", ("ls", 2 * (NV - 1) * n_out))
-    need("g", ("out0", 16))
-    need("g", ("out1", 16))
+    for s, val in (("rd", 32), ("rtl", 256), ("ls", 2 * (NV - 1) * n_out), ("out0", 16), ("out1", 16)):
+        need("g", (s, val))

@@ -7,12 +7,15 @@ NV = 5
 NRT = 1
 CHW = 64
 XCH = 64
-MISC = ((0, 128), (128, 256))
 NM = 35
 MQ, MW, MH, REV = 16, 22, 28, 34
 V = 2048
 LOOK = 0.05
-PEC = 0.0008
+PEC = 0.0007
+XFREE = (1,)
+VIA = (1, 3)
+BOOST = {'k0': 8, 's0': 10, 'm0': 6, 'n0': 4, 'l0': 6, 'e0': -4, 'g0': -3, 'w0': 4, 'g1': 2, 'm1': 2, 'cd': 2, 'cc': 1, 'k1': -1,
+         'ce': -1, 'r0': 2, 'g0z': -2, 't0z': 8, 'su': -2, 'wl': 2}
 
 f32, bf, fp, i32, u16 = "float32", "bfloat16", "float16", "int32", "uint16"
 SCRATCH = {"RD": ("dram", [8, 32, 1024], f32)}
@@ -21,13 +24,13 @@ for names, shape, d in (
         ("wd16", [128, 256], fp), ("rt16", [128, 1024], fp), ("RT0", [128, 1024], f32), ("RTR", [128, 16384], f32),
         ("RTab", [128, 4096], f32), ("NT", [128, 4352], f32), ("W0 W1 W2 W3 W4 S0 S1 S2 S3 rl ql", [128, 256], u16),
         ("w16 r16 q16 n16 qc h16 yf", [128, 256], fp), ("zi hi nv", [128, 256], i32),
-        ("xw X0 d", [128, 4096], bf), ("ad", [128, 16, 256], bf), ("Z hold", [128, 2048], bf),
+        ("xw X0 d", [128, 4096], bf), ("xg", [128, 1024], bf), ("ad", [128, 16, 256], bf), ("Z hold", [128, 2048], bf),
         ("row", [128, 144], i32), ("grow krow", [128, 128], i32), ("pc ki gi whi_i wlo_i aci acm", [128, 8], i32),
         ("ai gam", [128, 16], i32), ("pf kf gf g16 whi wlo thf kr15 ac a8", [128, 8], f32), ("bm oh", [128, 16], f32),
         ("tgt", [128, 560], i32), ("tga", [128, 256], i32), ("F1", [128, 35, 16], bf), ("CM", [128, 35, 160], bf),
         ("EZ ED WZh WZl", [128, 144], bf), ("BOb IB I4 IM ones", [128, 128], bf), ("c32", [128, 256], bf), ("BB", [128, 16, 128], bf),
         ("BO thr rs TH THe", [128, 128], f32), ("jrow", [128, 64], bf), ("okb hs", [128, 256], bf), ("km yo", [128, 256], f32),
-        ("ilf i8 tf at n2 s2 aj", [128, 16], f32), ("ilc fm rp", [128, 16], bf), ("uh ulo", [128, 16], fp),
+        ("ilf i8 tf at s2 aj", [128, 16], f32), ("ilc fm n2", [128, 16], bf), ("uh ulo", [128, 16], fp),
         ("ili ui uu zz cc u7 kk ks kq", [128, 16], i32), ("cl qo fl sl", [128, 16], u16)):
     for _n in names.split():
         SCRATCH[_n] = ("sbuf", shape, d)
@@ -65,7 +68,9 @@ def schedule(ops):
             succs[j].append((i, lat))
     prio = [0.0] * n
     for i in range(n - 1, -1, -1):
-        prio[i] = ops[i]["cost"] + ops[i]["lat"] + max([prio[j] + lat for j, lat in succs[i]] + [0.0])
+        c = ops[i]["cost"]
+        prio[i] = (min(c.values()) if ops[i]["q"] == "vs" else c) + ops[i]["lat"] + max([prio[j] + lat for j, lat in succs[i]] + [0.0])
+    prio = [prio[i] + ops[i]["boost"] for i in range(n)]
     left = [len(p) for p in preds]
     ready = [0.0] * n
     cand = {}
@@ -93,7 +98,7 @@ def schedule(ops):
             if i in c:
                 c.remove(i)
         if ops[i]["q"] == "vs":
-            ops[i]["q"], ops[i]["f"] = q, ops[i]["f"][q]
+            ops[i]["q"], ops[i]["f"], ops[i]["cost"] = q, ops[i]["f"][q], ops[i]["cost"][q]
         free[q] = st + ops[i]["cost"]
         order.append(i)
         for j, lat in succs[i]:
@@ -116,8 +121,17 @@ def rank_program(g, core, T, topo):
 
     ops = []
 
+    tag = [""]
+
     def op(q, fns, r, w, cost, lat=0.0, kind="c", sem=None):
-        ops.append({"q": q, "f": fns, "r": r, "w": w, "cost": cost, "lat": lat, "kind": kind, "sem": sem})
+        ops.append({"q": q, "f": fns, "r": r, "w": w, "cost": cost, "lat": lat, "kind": kind, "sem": sem, "boost": BOOST.get(tag[0], 0.0)})
+
+    def either(out, in_, scale, r, w, kv, ks):
+        if scale is None:
+            v, s = (lambda: vec.tensor_copy(out, in_)), (lambda: sca.activation(out, in_, ACT.Copy))
+        else:
+            v, s = (lambda: vec.tensor_scalar(out, in_, scale, None, ALU.mult)), (lambda: sca.activation(out, in_, ACT.Copy, scale=scale))
+        op("vs", {"v": [v], "s": [s]}, r, w, {"v": 0.06 + CY * max(64, kv), "s": 0.15 + CY * ks})
 
     CY = 0.00083
     A_ = lambda b, lo=0, hi=1 << 20: (b, lo, hi)
@@ -188,6 +202,7 @@ def rank_program(g, core, T, topo):
     tcopy(T.gf[:, 0:1], T.gi[:, 0:1], [A_("gi")], [A_("gf")], 1)
     ts(T.g16[:, 0:1], T.gf[:, 0:1], 16.0, 15.0, ALU.mult, ALU.add, [A_("gf")], [A_("g16")])
     ts(T.kr15[:, 0:1], T.kf[:, 0:1], -1.0, 15.0, ALU.mult, ALU.add, [A_("kf")], [A_("kr15")])
+    tag[0] = "ca"
     ts(T.tgt[:, 0:256], T.tga[:], 15, None, ALU.bitwise_and, None, [A_("tga")], [A_("tgt", 0, 256)], 256)
     ts(T.gam[:, 0:10], T.gam[:, 0:10], 7, None, ALU.bitwise_and, None, [A_("gam")], [A_("gam")])
     ts(T.bm[:, 0:10], T.gam[:, 0:10], T.gf[:, 0:1], None, ALU.is_equal, None, [A_("gam"), A_("gf")], [A_("bm")])
@@ -197,15 +212,13 @@ def rank_program(g, core, T, topo):
         for j in range(10):
             o, i_, sc = T.CM[:, m0:m1, 16 * j:16 * j + 16], T.F1[:, m0:m1, :], T.bm[:, j:j + 1]
             r, w = [A_("F1", m0, m1), A_("bm")], [A_("CM%d" % j, m0, m1)]
-            if m0 == 34 or (m0 == 16) == (j % 2 == 0):
-                ts(o, i_, sc, None, ALU.mult, None, r, w, 8 * (m1 - m0))
-            else:
-                actv(o, i_, ACT.Copy, r, w, 16 * (m1 - m0), scale=sc)
+            either(o, i_, sc, r, w, 8 * (m1 - m0), 16 * (m1 - m0))
 
     def cmat(m, rho):
         lo = 16 * (2 - rho)
         return T.CM[:, m, lo:lo + 128], [A_("CM%d" % j, m, m + 1) for j in range(2 - rho, 10 - rho)]
 
+    tag[0] = "cb"
     tcopy(T.wd16[:], T.wdi[:], [A_("wdi")], [A_("wd16")])
     c, rc = cmat(REV, 0)
     mms([(T.E0[:, 0:256], c, T.wd16[:], True, True)], rc + [A_("wd16")], [A_("E0")], 256)
@@ -220,6 +233,7 @@ def rank_program(g, core, T, topo):
     for s in range(16):
         dma("y", T.RTR[:, 1024 * s:1024 * s + 1024], T.RD[:, 16 - s:32 - s, :], [A_("RD")], [A_("RTR", s, s + 1)], "rtl", 256, 30.0)
 
+    tag[0] = "cc"
     ts(T.wlo_i[:, 0:1], T.wti[:, 0:1], 255, None, ALU.bitwise_and, None, [A_("wti")], [A_("wlo_i")])
     ts(T.whi_i[:, 0:1], T.wti[:, 0:1], 3840, None, ALU.bitwise_and, None, [A_("wti")], [A_("whi_i")])
     tcopy(T.wlo[:, 0:1], T.wlo_i[:, 0:1], [A_("wlo_i")], [A_("wlo")], 1)
@@ -241,24 +255,24 @@ def rank_program(g, core, T, topo):
     ts(T.i8[:], T.ilf[:], 8.0, None, ALU.mult, None, [A_("ilf")], [A_("i8")])
     ts(T.ilc[:, 0:8], T.ilf[:, 0:8], -128.0, None, ALU.add, None, [A_("ilf")], [A_("ilc")])
     irow = T.row[:, 0:128]
+    tag[0] = "cd"
     ri = [A_("row"), A_("pf")]
     ts(T.IB[:], irow, T.pf[:, 0:1], None, ALU.is_equal, None, ri, [A_("IB")], 128)
     ts(T.I4[:], irow, T.pf[:, 0:1], 4.0, ALU.is_equal, ALU.mult, ri, [A_("I4")], 128)
     ts(T.IM[:], irow, T.pf[:, 0:1], -1.0, ALU.is_equal, ALU.mult, ri, [A_("IM")], 128)
+    tag[0] = "ce"
     rg = [A_("grow"), A_("gf")]
     ts(T.BO[:], T.grow[:], T.gf[:, 0:1], None, ALU.is_equal, None, rg, [A_("BO")], 128)
     ts(T.BOb[:], T.grow[:], T.gf[:, 0:1], None, ALU.is_equal, None, rg, [A_("BOb")], 128)
     ts(T.oh[:], T.krow[:, 0:16], T.kf[:, 0:1], None, ALU.is_equal, None, [A_("krow"), A_("kf")], [A_("oh")])
     for b in range(16):
-        if b % 2:
-            ts(T.BB[:, b, :], T.BOb[:], T.oh[:, b:b + 1], None, ALU.mult, None, [A_("BOb"), A_("oh")], [A_("BB", b, b + 1)])
-        else:
-            actv(T.BB[:, b, :], T.BOb[:], ACT.Copy, [A_("BOb"), A_("oh")], [A_("BB", b, b + 1)], 128, scale=T.oh[:, b:b + 1])
+        either(T.BB[:, b, :], T.BOb[:], T.oh[:, b:b + 1], [A_("BOb"), A_("oh")], [A_("BB", b, b + 1)], 64, 128)
     tcopy(T.thf[:, 0:1], T.thi[:, 0:1], [A_("thi")], [A_("thf")], 1)
     ts(T.thr[:], T.krow[:], T.kr15[:, 0:1], T.thf[:, 0:1], ALU.is_equal, ALU.mult, [A_("krow"), A_("kr15"), A_("thf")], [A_("thr")], 128)
     mms([(T.L1[:, 0:128], T.BO[:], T.thr[:], True, True)], [A_("BO"), A_("thr")], [A_("L1")], 512)
     tcopy(T.TH[:], T.L1[:, 0:128], [A_("L1")], [A_("TH")], 128)
 
+    tag[0] = ""
     ebank = [0]
 
     def nextbank():
@@ -277,9 +291,10 @@ def rank_program(g, core, T, topo):
             lo, hi = ch * XCH, ch * XCH + XCH
             r, wr = [A_("xv", 0, V), A_(w, lo, hi)], [A_("xw", 16 * lo, 16 * hi)]
             out, win, off = T.xw[:, 16 * lo:16 * hi], T.xv[:, 0:V], T[w][:, lo:hi]
-            src = win.indirect(off)
-            op("vs", {"v": [(lambda o, s: lambda: vec.tensor_copy(o, s))(out, src)],
-                      "s": [(lambda o, s: lambda: sca.activation(o, s, ACT.Copy))(out, src)]}, r, wr, 0.1 + 24 * CY * XCH)
+            if ch in XFREE:
+                either(out, win.indirect(off), None, r, wr, 24 * XCH, 24 * XCH)
+            else:
+                actv(out, win.indirect(off), ACT.Copy, r, wr, 24 * XCH)
 
     def u_sum(h):
         P, lo = "P%d" % h, 2048 * h
@@ -293,7 +308,7 @@ def rank_program(g, core, T, topo):
     def expand(h):
         lo = 2048 * h
         R = lambda b: A_(b, lo, lo + 2048)
-        tcopy(T.Z[:, 0:2048:16], T.xw[:, lo + 15:lo + 2048:16], [R("xw")], [A_("Z")], 64)
+        either(T.Z[:, 0:2048:16], T.xw[:, lo + 15:lo + 2048:16], None, [R("xw")], [A_("Z")], 64, 128)
         scan(T.X0[:, lo:lo + 2048], T.hold[:], T.Z[:], 0.0, ALU.mult, ALU.add, [A_("hold"), A_("Z")], [R("X0")], 1024)
 
     def relators(t, h):
@@ -329,10 +344,18 @@ def rank_program(g, core, T, topo):
         for k in range(128 // CHW):
             w0 = 128 * h + k * CHW
             lo, hi, a0, a1 = 16 * w0, 16 * w0 + W16, w0 // 16, (w0 + CHW) // 16
+            if least and w0 // CHW in VIA:
+                actv(T.xg[:], T.xv[:, 0:V].indirect(T[lst][:, w0:w0 + CHW]), ACT.Copy, [A_("xv", 0, V), A_(lst, w0, w0 + CHW)], [A_("xg")], 1.5 * W16)
+                for z in range(0, W16, 512):
+                    e = nextbank()
+                    mms([(T[e][:], T.IB[:], T.xg[:, z:z + 512], True, False), (T[e][:], T.IM[:], T[other][:, lo + z:lo + z + 512], False, True)],
+                        [A_("IB"), A_("IM"), A_("xg"), A_(other, lo + z, lo + z + 512)], [A_(e)], 512)
+                    actv(T.ad[:, a0 + z // 256:a0 + z // 256 + 2, :], T[e][:], ACT.Abs, [A_(e)], [A_("ad", lo + z, lo + z + 512)], 512)
             d, win, off, x = T.d[:, lo:hi], T.xv[:, 0:V], T[lst][:, w0:w0 + CHW], T[other][:, lo:hi]
-            op("v", [(lambda d, win, off, x: lambda: vec.tensor_tensor(d, win.indirect(off), x, ALU.subtract))(d, win, off, x)],
-               [A_("xv", 0, V), A_(lst, w0, w0 + CHW), A_(other, lo, hi)], [A_("d", lo, hi)], 0.06 + 1.5 * CY * W16)
-            actv(T.ad[:, a0:a1, :], d, ACT.Abs, [A_("d", lo, hi)], [A_("ad", lo, hi)], W16)
+            if not (least and w0 // CHW in VIA):
+                op("v", [(lambda d, win, off, x: lambda: vec.tensor_tensor(d, win.indirect(off), x, ALU.subtract))(d, win, off, x)],
+                   [A_("xv", 0, V), A_(lst, w0, w0 + CHW), A_(other, lo, hi)], [A_("d", lo, hi)], 0.06 + 1.5 * CY * W16)
+                actv(T.ad[:, a0:a1, :], d, ACT.Abs, [A_("d", lo, hi)], [A_("ad", lo, hi)], W16)
             o = (128 if least else 256) + CHW * k
             out, E = T[P][:, o:o + CHW], ("ED" if least else "EZ")
             l = [(out, T.ones[0:1, :], T.jrow[0:1, 0:CHW], True, False)] if least else []
@@ -439,9 +462,8 @@ def rank_program(g, core, T, topo):
         op("v", [lambda: vec.tensor_copy(T.xv[:].indirect(T.sl[:]), T.nv[:])], [A_("sl"), A_("nv")], [A_("xv")], 0.7)
 
     def count():
-        ts(T.rp[:], T.hs[:, 15:256:16], 11.0, None, ALU.is_ge, None, [A_("hs")], [A_("rp")])
-        mms([(T.P0[:, 400:416], T.ones[:], T.rp[:], True, True)], [A_("ones"), A_("rp")], [A_("P0")])
-        actv(T.aj[:], T.P0[:, 400:416], ACT.Copy, [A_("P0")], [A_("aj"), A_("ac")], 16, accum_out=T.ac[:, 0:1])
+        mms([(T.P0[:, 400:416], T.ones[:], T.n2[:], True, True)], [A_("ones"), A_("n2")], [A_("P0")])
+        actv(T.aj[:], T.P0[:, 400:416], ACT.Copy, [A_("P0")], [A_("aj"), A_("ac")], 16, scale=-1.0 / 2048, accum_out=T.ac[:, 0:1])
         tcopy(T.aci[:, 0:1], T.ac[:, 0:1], [A_("ac")], [A_("aci")], 1)
         ts(T.acm[:, 0:1], T.aci[:, 0:1], 31, None, ALU.bitwise_and, None, [A_("aci")], [A_("acm")])
         ts(T.a8[:, 0:1], T.acm[:, 0:1], 8.0, None, ALU.mult, None, [A_("acm")], [A_("a8")])
@@ -451,38 +473,40 @@ def rank_program(g, core, T, topo):
     tcopy(T.THe[:], T.TH[:], [A_("TH")], [A_("THe")], 128)
     for t in range(NV):
         rho, W = GSH[t], "W%d" % t
+        def part(name, f, *args):
+            tag[0] = name + "z" if t == 0 and name + "z" in BOOST else name
+            f(*args)
+            tag[0] = ""
+
         for h in range(2):
+            s = str(h)
             w, RW = L128(h)
-            values(t, h)
-            u_sum(h)
-            expand(h)
-            relators(t, h)
-            tcopy(T.w16[:, w], T[W][:, w], [RW(W)], [RW("w16")], 64)
-            new_words(h, G[0], rho)
-            new_words(h, G[1], rho)
-            distances("rl", "X0", h, True)
+            part("x" + s, values, t, h)
+            part("u" + s, u_sum, h)
+            part("e" + s, expand, h)
+            part("r" + s, relators, t, h)
+            part("w" + s, tcopy, T.w16[:, w], T[W][:, w], [RW(W)], [RW("w16")], 64)
+            part("t" + s, new_words, h, G[0], rho)
+            part("t" + s, new_words, h, G[1], rho)
+            part("d" + s, distances, "rl", "X0", h, True)
             if t < NRT:
-                rotations(h)
-        spread_u()
-        at_list()
+                part("o" + s, rotations, h)
+        part("su", spread_u)
+        part("at", at_list)
         for h in range(2):
-            least(t, h)
-            for lo, hi in MISC:
-                if hi == 128 * h + 128:
-                    misc(lo, hi)
-            distances("ql", "xw", h, False)
-            new_values(h)
-            if hi == 256 and len(MISC) == 1 and h == 0:
-                continue
-            for k in ((0, 1) if len(MISC) == 1 else (h,)):
-                for j in (2, 3, 4):
-                    new_words(k, G[j], rho)
+            s = str(h)
+            part("l" + s, least, t, h)
+            part("m" + s, misc, 128 * h, 128 * h + 128)
+            part("g" + s, distances, "ql", "xw", h, False)
+            part("v" + s, new_values, h)
+            for j in (2, 3, 4):
+                part("n" + s, new_words, h, G[j], rho)
         for h in range(2):
-            match(h, rho)
-            send(t, h)
-        write_values()
+            part("k" + str(h), match, h, rho)
+            part("s" + str(h), send, t, h)
+        part("wl", write_values)
         if t < NV - 1:
-            count()
+            part("ct", count)
 
     dma("y", T.yx[:], T.xv[:, 0:V], [A_("xv", 0, V)], [], "out0", 16, 5.0)
     c, rc = cmat(REV, 0)

from concourse.bass import DstId, RemoteDMATransfer
from concourse.mybir import dt, AluOpType, AxisListType, ActivationFunctionType

ALU = AluOpType
ACT = ActivationFunctionType
NV = 5
NRT = 1
CHW = 64
XCH = 64
NM = 35
MQ, MW, MH, REV = 16, 22, 28, 34
V = 2048
LOOK = 0.05
PEC = 0.0007
XFREE = (1,)
VIA = (1, 3)
BOOST = {'k0': 8, 's0': 10, 'm0': 6, 'n0': 4, 'l0': 6, 'e0': -4, 'g0': -3, 'w0': 4, 'g1': 2, 'm1': 2, 'cd': 2, 'cc': 1, 'k1': -1,
         'ce': -1, 'r0': 2, 'g0z': -2, 't0z': 8, 'su': -2, 'wl': 2}

f32, bf, fp, i32, u16 = "float32", "bfloat16", "float16", "int32", "uint16"
SCRATCH = {"RD": ("dram", [8, 32, 1024], f32)}
for names, shape, d in (
        ("xv", [128, 4096], bf), ("wdi", [128, 256], i32), ("rti", [128, 1024], i32), ("wti thi", [128, 8], i32),
        ("wd16", [128, 256], fp), ("rt16", [128, 1024], fp), ("RT0", [128, 1024], f32), ("RTR", [128, 16384], f32),
        ("RTab", [128, 4096], f32), ("NT", [128, 4352], f32), ("W0 W1 W2 W3 W4 S0 S1 S2 S3 rl ql", [128, 256], u16),
        ("w16 r16 q16 n16 qc h16 yf", [128, 256], fp), ("zi hi nv", [128, 256], i32),
        ("xw X0 d", [128, 4096], bf), ("xg", [128, 1024], bf), ("ad", [128, 16, 256], bf), ("Z hold", [128, 2048], bf),
        ("row", [128, 144], i32), ("grow krow", [128, 128], i32), ("pc ki gi whi_i wlo_i aci acm", [128, 8], i32),
        ("ai gam", [128, 16], i32), ("pf kf gf g16 whi wlo thf kr15 ac a8", [128, 8], f32), ("bm oh", [128, 16], f32),
        ("tgt", [128, 560], i32), ("tga", [128, 256], i32), ("F1", [128, 35, 16], bf), ("CM", [128, 35, 160], bf),
        ("EZ ED WZh WZl", [128, 144], bf), ("BOb IB I4 IM ones", [128, 128], bf), ("c32", [128, 256], bf), ("BB", [128, 16, 128], bf),
        ("BO thr rs TH THe", [128, 128], f32), ("jrow", [128, 64], bf), ("okb hs", [128, 256], bf), ("km yo", [128, 256], f32),
        ("ilf i8 tf at s2 aj", [128, 16], f32), ("ilc fm n2", [128, 16], bf), ("uh ulo", [128, 16], fp),
        ("ili ui uu zz cc u7 kk ks kq", [128, 16], i32), ("cl qo fl sl", [128, 16], u16)):
    for _n in names.split():
        SCRATCH[_n] = ("sbuf", shape, d)
PSUM = ("P0", "P1", "L0", "L1", "E0", "E1", "E2", "E3")
for _n in PSUM:
    SCRATCH[_n] = ("psum", [128, 512], f32)
SEMAPHORES = (["qv", "qs", "qt", "qg", "ls"] + ["ld%d" % k for k in range(6)] + ["rd", "rtl", "out0", "out1"]
              + ["ar%d_%d" % (t, h) for t in range(1, NV) for h in range(2)])
GSH = [(t + t // 4) - (t - 1 + (t - 1) // 4) for t in range(1, NV)] + [0]


def schedule(ops):
    wake, hist, n = 0.1, {}, len(ops)
    preds, succs = [{} for _ in ops], [[] for _ in ops]
    for i, o in enumerate(ops):
        q = o["q"]
        for regs, wr in ((o["r"], False), (o["w"], True)):
            for b, lo, hi in regs:
                for l2, h2, j, w2 in hist.get(b, ()):
                    if j == i or (b not in PSUM and (l2 >= hi or h2 <= lo or not (wr or w2))):
                        continue
                    lat = wake if (ops[j]["q"] != q or b not in PSUM or ops[j]["lat"]) else 0.0
                    preds[i][j] = max(preds[i].get(j, 0.0), lat)
        for regs, wr in ((o["r"], False), (o["w"], True)):
            for b, lo, hi in regs:
                if b in PSUM:
                    hist[b] = [(lo, hi, i, True)]
                else:
                    old = hist.get(b, [])
                    if wr:
                        old = [e for e in old if not (e[0] >= lo and e[1] <= hi)]
                    hist[b] = old + [(lo, hi, i, wr)]
    for i in range(n):
        for j, lat in preds[i].items():
            succs[j].append((i, lat))
    prio = [0.0] * n
    for i in range(n - 1, -1, -1):
        c = ops[i]["cost"]
        prio[i] = (min(c.values()) if ops[i]["q"] == "vs" else c) + ops[i]["lat"] + max([prio[j] + lat for j, lat in succs[i]] + [0.0])
    prio = [prio[i] + ops[i]["boost"] for i in range(n)]
    left = [len(p) for p in preds]
    ready = [0.0] * n
    cand = {}

    def enter(i):
        for q in (("s", "v") if ops[i]["q"] == "vs" else (ops[i]["q"],)):
            cand.setdefault(q, []).append(i)

    for i in range(n):
        if not left[i]:
            enter(i)
    free, order = {}, []
    while len(order) < n:
        best = None
        for q, c in cand.items():
            if not c:
                continue
            t0 = min(max(free.get(q, 0.0), ready[i]) for i in c)
            k = max((i for i in c if max(free.get(q, 0.0), ready[i]) <= t0 + LOOK), key=lambda i: (prio[i], -i))
            st = max(free.get(q, 0.0), ready[k])
            if best is None or st < best[0]:
                best = (st, k, q)
        st, i, q = best
        for c in cand.values():
            if i in c:
                c.remove(i)
        if ops[i]["q"] == "vs":
            ops[i]["q"], ops[i]["f"], ops[i]["cost"] = q, ops[i]["f"][q], ops[i]["cost"][q]
        free[q] = st + ops[i]["cost"]
        order.append(i)
        for j, lat in succs[i]:
            ready[j] = max(ready[j], free[q] + ops[i]["lat"] + lat)
            left[j] -= 1
            if not left[j]:
                enter(j)
    return order


def rank_program(g, core, T, topo):
    rank = T.rank_of(core)
    if rank is None:
        return
    n = len(T.cores)
    nxt, prv = T.cores[(rank + 1) % n], T.cores[(rank - 1) % n]
    out_engines = topo.engines(core, nxt)[:8]
    smask, n_out = sum(1 << e for e in out_engines), len(out_engines)
    n_in = len(topo.engines(prv, core)[:8])

    ops = []

    tag = [""]

    def op(q, fns, r, w, cost, lat=0.0, kind="c", sem=None):
        ops.append({"q": q, "f": fns, "r": r, "w": w, "cost": cost, "lat": lat, "kind": kind, "sem": sem, "boost": BOOST.get(tag[0], 0.0)})

    def either(out, in_, scale, r, w, kv, ks):
        if scale is None:
            v, s = (lambda: vec.tensor_copy(out, in_)), (lambda: sca.activation(out, in_, ACT.Copy))
        else:
            v, s = (lambda: vec.tensor_scalar(out, in_, scale, None, ALU.mult)), (lambda: sca.activation(out, in_, ACT.Copy, scale=scale))
        op("vs", {"v": [v], "s": [s]}, r, w, {"v": 0.06 + CY * max(64, kv), "s": 0.15 + CY * ks})

    CY = 0.00083
    A_ = lambda b, lo=0, hi=1 << 20: (b, lo, hi)
    vec, sca, ten = g.vector, g.scalar, g.tensor

    def tcopy(out, in_, r, w, k=256):
        op("v", [lambda: vec.tensor_copy(out, in_)], r, w, 0.06 + CY * max(64, k))

    def vgather(out, win, off, r, w, k):
        op("v", [lambda: vec.tensor_copy(out, win.indirect(off))], r, w, 0.06 + 1.5 * CY * k)

    def tt(out, a, b, o, r, w, k=64):
        op("v", [lambda: vec.tensor_tensor(out, a, b, o)], r, w, 0.06 + CY * max(64, k))

    def ts(out, a, s1, s2, o0, o1, r, w, k=64):
        if o1 is None:
            op("v", [lambda: vec.tensor_scalar(out, a, s1, None, o0)], r, w, 0.06 + CY * max(64, k))
        else:
            op("v", [lambda: vec.tensor_scalar(out, a, s1, s2, o0, o1)], r, w, 0.06 + CY * max(64, k))

    def scan(out, d0, d1, init, o0, o1, r, w, k):
        op("v", [lambda: vec.tensor_tensor_scan(out, d0, d1, init, o0, o1)], r, w, 0.06 + CY * k)

    def mset(ap, c, w, k, r=()):
        op("v", [lambda: vec.memset(ap, c)], list(r), w, 0.06 + CY * max(64, k))

    def actv(out, in_, f, r, w, k, **kw):
        op("s", [lambda: sca.activation(out, in_, f, **kw)], r, w, 0.18 + CY * k)

    def mms(lst, r, w, cols=64):
        op("t", [(lambda a: lambda: ten.matmul(*a))(a) for a in lst], r, w, len(lst) * PEC * cols)

    def iota(out, pat, base, cm, w, k=16):
        op("g", [lambda: g.iota(out, pat, base, cm)], [], w, 0.13 + 2 * CY * k)

    def dma(q, out, in_, r, w, sem, total, lat):
        eng = {"y": g.sync, "s": sca}[q]
        op(q, [lambda: eng.dma_start(out, in_)], r, w, 0.07, lat, "d", (sem, total))

    dma("s", T.wdi[:], T.wd[:], [], [A_("wdi")], "ld0", 16, 2.5)
    dma("y", T.xv[:, 0:V], T.x[:], [], [A_("xv", 0, V)], "ld1", 16, 5.0)
    dma("s", T.rti[:, 712:1024], T.rt[:, 0:312], [], [A_("rti", 712, 1024)], "ld2", 16, 4.0)
    dma("s", T.rti[:, 0:712], T.rt[:, 312:1024], [], [A_("rti", 0, 712)], "ld3", 16, 5.0)
    dma("s", T.wti[:, 0:1], T.wt[:], [], [A_("wti")], "ld4", 16, 4.0)
    dma("s", T.thi[:, 0:1], T.th[:], [], [A_("thi")], "ld5", 16, 5.0)

    iota(T.pc[:, 0:1], [[1, 1]], 0, 1, [A_("pc")])
    iota(T.tga[:], [[-1, 16], [1, 16]], 16, 0, [A_("tga")], 256)
    iota(T.gam[:, 0:10], [[1, 10]], 6, 0, [A_("gam")])
    mset(T.tgt[:, 256:560], -1, [A_("tgt", 256, 560)], 304)
    iota(T.tgt[:, REV * 16:REV * 16 + 16], [[-1, 16]], 15, 0, [A_("tgt", REV * 16, REV * 16 + 16)])
    for l in range(10, 16):
        a = (MQ + l - 10) * 16
        iota(T.tgt[:, a + l:a + 16], [[-1, 16 - l]], 15 - l, 0, [A_("tgt", a + l, a + 16)])
        a = (MW + l - 10) * 16
        iota(T.tgt[:, a + 2 * l - 16:a + l], [[1, 16 - l]], 0, 0, [A_("tgt", a + 2 * l - 16, a + l)])
        a = (MH + l - 10) * 16
        iota(T.tgt[:, a:a + 2 * l - 16], [[1, 2 * l - 16]], 0, 0, [A_("tgt", a, a + 2 * l - 16)])
    iota(T.row[:, 0:144], [[1, 144]], 0, 0, [A_("row")], 144)
    iota(T.grow[:], [[1, 8], [0, 16]], 0, 0, [A_("grow")], 128)
    iota(T.krow[:], [[0, 8], [1, 16]], 0, 0, [A_("krow")], 128)
    iota(T.ai[:], [[16, 16]], 0, 0, [A_("ai")])

    ts(T.ki[:, 0:1], T.pc[:, 0:1], 15, None, ALU.bitwise_and, None, [A_("pc")], [A_("ki")])
    ts(T.gi[:, 0:1], T.pc[:, 0:1], 4, None, ALU.logical_shift_right, None, [A_("pc")], [A_("gi")])
    tcopy(T.pf[:, 0:1], T.pc[:, 0:1], [A_("pc")], [A_("pf")], 1)
    tcopy(T.kf[:, 0:1], T.ki[:, 0:1], [A_("ki")], [A_("kf")], 1)
    tcopy(T.gf[:, 0:1], T.gi[:, 0:1], [A_("gi")], [A_("gf")], 1)
    ts(T.g16[:, 0:1], T.gf[:, 0:1], 16.0, 15.0, ALU.mult, ALU.add, [A_("gf")], [A_("g16")])
    ts(T.kr15[:, 0:1], T.kf[:, 0:1], -1.0, 15.0, ALU.mult, ALU.add, [A_("kf")], [A_("kr15")])
    tag[0] = "ca"
    ts(T.tgt[:, 0:256], T.tga[:], 15, None, ALU.bitwise_and, None, [A_("tga")], [A_("tgt", 0, 256)], 256)
    ts(T.gam[:, 0:10], T.gam[:, 0:10], 7, None, ALU.bitwise_and, None, [A_("gam")], [A_("gam")])
    ts(T.bm[:, 0:10], T.gam[:, 0:10], T.gf[:, 0:1], None, ALU.is_equal, None, [A_("gam"), A_("gf")], [A_("bm")])
    for m0, m1 in ((34, 35), (0, 16), (16, 34)):
        ts(T.F1[:, m0:m1, :], T.tgt[:, 16 * m0:16 * m1], T.kf[:, 0:1], None, ALU.is_equal, None,
           [A_("tgt", 16 * m0, 16 * m1), A_("kf")], [A_("F1", m0, m1)], 16 * (m1 - m0))
        for j in range(10):
            o, i_, sc = T.CM[:, m0:m1, 16 * j:16 * j + 16], T.F1[:, m0:m1, :], T.bm[:, j:j + 1]
            r, w = [A_("F1", m0, m1), A_("bm")], [A_("CM%d" % j, m0, m1)]
            either(o, i_, sc, r, w, 8 * (m1 - m0), 16 * (m1 - m0))

    def cmat(m, rho):
        lo = 16 * (2 - rho)
        return T.CM[:, m, lo:lo + 128], [A_("CM%d" % j, m, m + 1) for j in range(2 - rho, 10 - rho)]

    tag[0] = "cb"
    tcopy(T.wd16[:], T.wdi[:], [A_("wdi")], [A_("wd16")])
    c, rc = cmat(REV, 0)
    mms([(T.E0[:, 0:256], c, T.wd16[:], True, True)], rc + [A_("wd16")], [A_("E0")], 256)
    tcopy(T.W0[:], T.E0[:, 0:256], [A_("E0")], [A_("W0")])
    for k, e in ((0, "E1"), (1, "E2")):
        s = slice(512 * k, 512 * k + 512)
        tcopy(T.rt16[:, s], T.rti[:, s], [A_("rti", s.start, s.stop)], [A_("rt16", s.start, s.stop)], 512)
        mms([(T[e][:], c, T.rt16[:, s], True, True)], rc + [A_("rt16", s.start, s.stop)], [A_(e)], 512)
        actv(T.RT0[:, s], T[e][:], ACT.Copy, [A_(e)], [A_("RT0", s.start, s.stop)], 512)
    dma("y", T.RD[:, 0:16, :], T.RT0[:], [A_("RT0")], [A_("RD", 0, 1)], "rd", 32, 5.0)
    dma("y", T.RD[:, 16:32, :], T.RT0[:], [A_("RT0")], [A_("RD", 1, 2)], "rd", 32, 8.0)
    for s in range(16):
        dma("y", T.RTR[:, 1024 * s:1024 * s + 1024], T.RD[:, 16 - s:32 - s, :], [A_("RD")], [A_("RTR", s, s + 1)], "rtl", 256, 30.0)

    tag[0] = "cc"
    ts(T.wlo_i[:, 0:1], T.wti[:, 0:1], 255, None, ALU.bitwise_and, None, [A_("wti")], [A_("wlo_i")])
    ts(T.whi_i[:, 0:1], T.wti[:, 0:1], 3840, None, ALU.bitwise_and, None, [A_("wti")], [A_("whi_i")])
    tcopy(T.wlo[:, 0:1], T.wlo_i[:, 0:1], [A_("wlo_i")], [A_("wlo")], 1)
    tcopy(T.whi[:, 0:1], T.whi_i[:, 0:1], [A_("whi_i")], [A_("whi")], 1)
    sel = [A_("row"), A_("g16")]
    ts(T.WZh[:], T.row[:], T.g16[:, 0:1], T.whi[:, 0:1], ALU.is_equal, ALU.mult, sel + [A_("whi")], [A_("WZh")], 144)
    ts(T.WZl[:], T.row[:], T.g16[:, 0:1], T.wlo[:, 0:1], ALU.is_equal, ALU.mult, sel + [A_("wlo")], [A_("WZl")], 144)
    ts(T.ED[:], T.row[:], T.g16[:, 0:1], 16384.0, ALU.is_equal, ALU.mult, sel, [A_("ED")], 144)
    ts(T.EZ[:], T.row[:], T.g16[:, 0:1], None, ALU.is_equal, None, sel, [A_("EZ")], 144)
    mset(T.Z[:], 0.0, [A_("Z")], 1024)
    mset(T.hold[:], 1.0, [A_("hold")], 1024)
    mset(T.hold[:, 0:2048:16], 0.0, [A_("hold")], 64, [A_("hold")])
    mset(T.ones[:], 1.0, [A_("ones")], 64)
    mset(T.c32[:], 32.0, [A_("c32")], 64)
    ts(T.jrow[:], T.krow[:, 0:64], -1024.0, 15360.0, ALU.mult, ALU.add, [A_("krow")], [A_("jrow")])
    ts(T.rs[:], T.krow[:], 0.0, 1e9, ALU.is_equal, ALU.mult, [A_("krow")], [A_("rs")], 128)
    ts(T.ilf[:], T.ai[:], T.kf[:, 0:1], None, ALU.add, None, [A_("ai"), A_("kf")], [A_("ilf")])
    tcopy(T.ili[:], T.ilf[:], [A_("ilf")], [A_("ili")], 16)
    ts(T.i8[:], T.ilf[:], 8.0, None, ALU.mult, None, [A_("ilf")], [A_("i8")])
    ts(T.ilc[:, 0:8], T.ilf[:, 0:8], -128.0, None, ALU.add, None, [A_("ilf")], [A_("ilc")])
    irow = T.row[:, 0:128]
    tag[0] = "cd"
    ri = [A_("row"), A_("pf")]
    ts(T.IB[:], irow, T.pf[:, 0:1], None, ALU.is_equal, None, ri, [A_("IB")], 128)
    ts(T.I4[:], irow, T.pf[:, 0:1], 4.0, ALU.is_equal, ALU.mult, ri, [A_("I4")], 128)
    ts(T.IM[:], irow, T.pf[:, 0:1], -1.0, ALU.is_equal, ALU.mult, ri, [A_("IM")], 128)
    tag[0] = "ce"
    rg = [A_("grow"), A_("gf")]
    ts(T.BO[:], T.grow[:], T.gf[:, 0:1], None, ALU.is_equal, None, rg, [A_("BO")], 128)
    ts(T.BOb[:], T.grow[:], T.gf[:, 0:1], None, ALU.is_equal, None, rg, [A_("BOb")], 128)
    ts(T.oh[:], T.krow[:, 0:16], T.kf[:, 0:1], None, ALU.is_equal, None, [A_("krow"), A_("kf")], [A_("oh")])
    for b in range(16):
        either(T.BB[:, b, :], T.BOb[:], T.oh[:, b:b + 1], [A_("BOb"), A_("oh")], [A_("BB", b, b + 1)], 64, 128)
    tcopy(T.thf[:, 0:1], T.thi[:, 0:1], [A_("thi")], [A_("thf")], 1)
    ts(T.thr[:], T.krow[:], T.kr15[:, 0:1], T.thf[:, 0:1], ALU.is_equal, ALU.mult, [A_("krow"), A_("kr15"), A_("thf")], [A_("thr")], 128)
    mms([(T.L1[:, 0:128], T.BO[:], T.thr[:], True, True)], [A_("BO"), A_("thr")], [A_("L1")], 512)
    tcopy(T.TH[:], T.L1[:, 0:128], [A_("L1")], [A_("TH")], 128)

    tag[0] = ""
    ebank = [0]

    def nextbank():
        ebank[0] = (ebank[0] + 1) % 4
        return "E%d" % ebank[0]

    def T8(h):
        return slice(8 * h, 8 * h + 8), (lambda b: A_(b, 8 * h, 8 * h + 8))

    def L128(h):
        return slice(128 * h, 128 * h + 128), (lambda b: A_(b, 128 * h, 128 * h + 128))

    def values(t, h):
        w = "W%d" % t
        for ch in range(128 * h // XCH, 128 * (h + 1) // XCH):
            lo, hi = ch * XCH, ch * XCH + XCH
            r, wr = [A_("xv", 0, V), A_(w, lo, hi)], [A_("xw", 16 * lo, 16 * hi)]
            out, win, off = T.xw[:, 16 * lo:16 * hi], T.xv[:, 0:V], T[w][:, lo:hi]
            if ch in XFREE:
                either(out, win.indirect(off), None, r, wr, 24 * XCH, 24 * XCH)
            else:
                actv(out, win.indirect(off), ACT.Copy, r, wr, 24 * XCH)

    def u_sum(h):
        P, lo = "P%d" % h, 2048 * h
        l = []
        for b in range(16):
            rhs = T.xw[:, lo + 16 * b + 15:lo + 2048:256]
            l.append((T[P][:, 0:8], T.WZh[:, 15 - b:143 - b], rhs, b == 0, False))
            l.append((T[P][:, 0:8], T.WZl[:, 15 - b:143 - b], rhs, False, b == 15))
        mms(l, [A_("xw", lo, lo + 2048), A_("WZh"), A_("WZl")], [A_(P)])

    def expand(h):
        lo = 2048 * h
        R = lambda b: A_(b, lo, lo + 2048)
        either(T.Z[:, 0:2048:16], T.xw[:, lo + 15:lo + 2048:16], None, [R("xw")], [A_("Z")], 64, 128)
        scan(T.X0[:, lo:lo + 2048], T.hold[:], T.Z[:], 0.0, ALU.mult, ALU.add, [A_("hold"), A_("Z")], [R("X0")], 1024)

    def relators(t, h):
        P = "P%d" % h
        c8, R = T8(h)
        w, RW = L128(h)
        tcopy(T.ui[:, c8], T[P][:, 0:8], [A_(P)], [R("ui")], 8)
        ts(T.uu[:, c8], T.ui[:, c8], 4095, None, ALU.bitwise_and, None, [R("ui")], [R("uu")])
        ts(T.tf[:, c8], T.uu[:, c8], 592.0, None, ALU.add, None, [R("uu")], [R("tf")])
        tt(T.zz[:, c8], T.tf[:, c8], T.tf[:, c8], ALU.mult, [R("tf")], [R("zz")])
        ts(T.cc[:, c8], T.zz[:, c8], 5, 1023, ALU.logical_shift_right, ALU.bitwise_and, [R("zz")], [R("cc")])
        tcopy(T.cl[:, c8], T.cc[:, c8], [R("cc")], [R("cl")], 8)
        vgather(T.rl[:, w], T.RT0[:], T.cl[:, c8], [A_("RT0"), R("cl")], [RW("rl")], 128)
        if t < NRT:
            tcopy(T.r16[:, w], T.rl[:, w], [RW("rl")], [RW("r16")], 64)

    def spread_u():
        tcopy(T.uh[:], T.uu[:], [A_("uu")], [A_("uh")], 16)
        tt(T.ulo[:], T.uu[:], T.uh[:], ALU.subtract, [A_("uu"), A_("uh")], [A_("ulo")])
        l = [(T.L0[:, 0:256], T.IB[:], T.c32[:], True, False)]
        for b in range(16):
            out = T.L0[:, b:256:16]
            l.append((out, T.BB[:, b, :], T.uh[:], False, False))
            l.append((out, T.BB[:, b, :], T.ulo[:], False, b == 15))
        mms(l, [A_("IB"), A_("c32"), A_("BB"), A_("uh"), A_("ulo")], [A_("L0")])

    def at_list():
        ts(T.u7[:], T.ui[:], 7, None, ALU.bitwise_and, None, [A_("ui")], [A_("u7")])
        tt(T.at[:], T.u7[:], T.i8[:], ALU.add, [A_("u7"), A_("i8")], [A_("at")])

    def distances(lst, other, h, least):
        P, W16 = "P%d" % h, 16 * CHW
        for k in range(128 // CHW):
            w0 = 128 * h + k * CHW
            lo, hi, a0, a1 = 16 * w0, 16 * w0 + W16, w0 // 16, (w0 + CHW) // 16
            if least and w0 // CHW in VIA:
                actv(T.xg[:], T.xv[:, 0:V].indirect(T[lst][:, w0:w0 + CHW]), ACT.Copy, [A_("xv", 0, V), A_(lst, w0, w0 + CHW)], [A_("xg")], 1.5 * W16)
                for z in range(0, W16, 512):
                    e = nextbank()
                    mms([(T[e][:], T.IB[:], T.xg[:, z:z + 512], True, False), (T[e][:], T.IM[:], T[other][:, lo + z:lo + z + 512], False, True)],
                        [A_("IB"), A_("IM"), A_("xg"), A_(other, lo + z, lo + z + 512)], [A_(e)], 512)
                    actv(T.ad[:, a0 + z // 256:a0 + z // 256 + 2, :], T[e][:], ACT.Abs, [A_(e)], [A_("ad", lo + z, lo + z + 512)], 512)
            d, win, off, x = T.d[:, lo:hi], T.xv[:, 0:V], T[lst][:, w0:w0 + CHW], T[other][:, lo:hi]
            if not (least and w0 // CHW in VIA):
                op("v", [(lambda d, win, off, x: lambda: vec.tensor_tensor(d, win.indirect(off), x, ALU.subtract))(d, win, off, x)],
                   [A_("xv", 0, V), A_(lst, w0, w0 + CHW), A_(other, lo, hi)], [A_("d", lo, hi)], 0.06 + 1.5 * CY * W16)
                actv(T.ad[:, a0:a1, :], d, ACT.Abs, [A_("d", lo, hi)], [A_("ad", lo, hi)], W16)
            o = (128 if least else 256) + CHW * k
            out, E = T[P][:, o:o + CHW], ("ED" if least else "EZ")
            l = [(out, T.ones[0:1, :], T.jrow[0:1, 0:CHW], True, False)] if least else []
            for b in range(16):
                l.append((out, T[E][:, 15 - b:143 - b], T.ad[:, a0:a1, 16 * b:16 * b + 16], b == 0 and not least, b == 15))
            mms(l, [A_("ones"), A_("jrow"), A_(E), A_("ad", lo, hi)], [A_(P)])

    def rotations(h):
        w, RW = L128(h)
        for q4 in range(4):
            e = nextbank()
            l, r = [], [RW("r16")]
            for j in range(4):
                c, rc = cmat(4 * q4 + j, 0)
                r += rc
                l.append((T[e][:, 128 * j:128 * j + 128], c, T.r16[:, w], True, True))
            mms(l, r, [A_(e)], 128)
            lo = 2048 * h + 512 * q4
            actv(T.RTab[:, lo:lo + 512], T[e][:], ACT.Copy, [A_(e)], [A_("RTab", lo, lo + 512)], 512)

    def least(t, h):
        P = "P%d" % h
        c8, R = T8(h)
        w, RW = L128(h)
        scan(T.km[:, w], T.rs[:], T[P][:, 128:256], 0.0, ALU.max, ALU.min, [A_("rs"), A_(P)], [RW("km")], 128)
        tcopy(T.kk[:, c8], T.km[:, 128 * h + 15:128 * h + 128:16], [RW("km")], [R("kk")], 8)
        if t < NRT:
            ts(T.ks[:, c8], T.kk[:, c8], 15360, 3, ALU.bitwise_and, ALU.logical_shift_right, [R("kk")], [R("ks")])
            tt(T.kq[:, c8], T.ks[:, c8], T.ili[:, 0:8], ALU.add, [R("ks"), A_("ili")], [R("kq")])
            win, rw = T.RTab[:, 2048 * h:2048 * h + 2048], A_("RTab", 2048 * h, 2048 * h + 2048)
        else:
            ts(T.ks[:, c8], T.kk[:, c8], 15360, None, ALU.bitwise_and, None, [R("kk")], [R("ks")])
            tt(T.kq[:, c8], T.ks[:, c8], T.cc[:, c8], ALU.add, [R("ks"), R("cc")], [R("kq")])
            win, rw = T.RTR[:], A_("RTR")
        tcopy(T.qo[:, c8], T.kq[:, c8], [R("kq")], [R("qo")], 8)
        vgather(T.ql[:, w], win, T.qo[:, c8], [rw, R("qo")], [RW("ql")], 128)

    def misc(lo, hi):
        w, k = slice(lo, hi), hi - lo
        RW = lambda b: A_(b, lo, hi)
        tcopy(T.q16[:, w], T.ql[:, w], [RW("ql")], [RW("q16")], k // 2)
        ts(T.n16[:, w], T.ql[:, w], 0.5, 1023.8, ALU.mult, ALU.add, [RW("ql")], [RW("n16")], k // 2)
        mms([(T.L1[:, w], T.I4[:], T.n16[:, w], True, False), (T.L1[:, w], T.IM[:], T.q16[:, w], False, True)],
            [A_("I4"), A_("IM"), RW("n16"), RW("q16")], [A_("L1")], k)
        tt(T.zi[:, w], T.L0[:, w], T.q16[:, w], ALU.mult, [RW("q16"), A_("L0")], [RW("zi")], k)
        ts(T.hi[:, w], T.zi[:, w], 5, 2047, ALU.logical_shift_right, ALU.bitwise_and, [RW("zi")], [RW("hi")], k)
        ts(T.qc[:, w], T.L1[:, w], -4095.0, None, ALU.add, None, [A_("L1")], [RW("qc")], k)
        tcopy(T.h16[:, w], T.hi[:, w], [RW("hi")], [RW("h16")], k)

    def new_words(h, lens, rho):
        e = nextbank()
        w, RW = L128(h)
        ls, r = [], []
        for j, l in enumerate(lens):
            if l < 10:
                parts = [(l + 1, "w16")]
            elif l == 16:
                parts = [(0, "h16")]
            else:
                parts = [(MW + l - 10, "w16"), (MQ + l - 10, "qc"), (MH + l - 10, "h16")]
            for k, (m, src) in enumerate(parts):
                c, rc = cmat(m, rho)
                r += rc + [RW(src)]
                ls.append((T[e][:, 128 * j:128 * j + 128], c, T[src][:, w], k == 0, k == len(parts) - 1))
        mms(ls, r, [A_(e)], 128)
        lo, sz = 2176 * h + 128 * lens[0], 128 * len(lens)
        actv(T.NT[:, lo:lo + sz], T[e][:, 0:sz], ACT.Copy, [A_(e)], [A_("NT", lo, lo + sz)], sz)

    def match(h, rho):
        P = "P%d" % h
        c8, R = T8(h)
        w, RW = L128(h)
        tt(T.okb[:, w], T[P][:, 256:384], T.THe[:], ALU.is_le, [A_(P), A_("THe")], [RW("okb")], 128)
        scan(T.hs[:, w], T.okb[:, w], T.ones[:], 1.0, ALU.mult, ALU.add, [RW("okb"), A_("ones")], [RW("hs")], 64)
        ts(T.fm[:, c8], T.hs[:, 128 * h + 15:128 * h + 128:16], 17.0, 128.0, ALU.min, ALU.mult, [RW("hs")], [R("fm")])
        c, rc = cmat(0, rho)
        mms([(T[P][:, 384:392], c, T.fm[:, c8], True, False), (T[P][:, 384:392], T.IB[:], T.ilc[:, 0:8], False, True)],
            rc + [A_("IB"), A_("ilc"), R("fm")], [A_(P)])
        tcopy(T.fl[:, c8], T[P][:, 384:392], [A_(P)], [R("fl")], 8)

    def send(t, h):
        c8, R = T8(h)
        w, RW = L128(h)
        out, lo = ("S%d" % t if t < NV - 1 else "yf"), 2176 * h
        vgather(T[out][:, w], T.NT[:, lo:lo + 2176], T.fl[:, c8], [A_("NT", lo, lo + 2176), R("fl")], [RW(out)], 128)
        if t < NV - 1:
            rid, pid = topo.addr(nxt, core)
            dst, src, sem = T["W%d" % (t + 1)][:, w], T[out][:, w], T.sem["ar%d_%d" % (t + 1, h)]
            op("g", [lambda: g.remote_dma(dst, src, sem, T.sem.ls, pid, rid, smask)], [RW(out)], [RW("W%d" % (t + 1))], 0.3, 2.6, "r")

    def new_values(h):
        lo = 2048 * h
        w, RW = L128(h)
        out = T.L1[:, 256 + 128 * h:384 + 128 * h]
        mms([(out, T.IB[:], T.xw[:, lo + 15:lo + 2048:16], True, False), (out, T.IB[:], T.xw[:, lo:lo + 2048:16], False, False),
             (out, T.IB[:], T.d[:, lo:lo + 2048:16], False, True)],
            [A_("IB"), A_("xw", lo, lo + 2048), A_("d", lo, lo + 2048)], [A_("L1")], 128)
        ts(T.nv[:, w], out, 0.5, -0.25, ALU.mult, ALU.add, [A_("L1")], [RW("nv")], 128)

    def write_values():
        ts(T.n2[:], T.hs[:, 15:256:16], 11.0, 2048.0, ALU.is_lt, ALU.mult, [A_("hs")], [A_("n2")])
        tt(T.s2[:], T.n2[:], T.at[:], ALU.add, [A_("n2"), A_("at")], [A_("s2")])
        tcopy(T.sl[:], T.s2[:], [A_("s2")], [A_("sl")], 16)
        op("v", [lambda: vec.tensor_copy(T.xv[:].indirect(T.sl[:]), T.nv[:])], [A_("sl"), A_("nv")], [A_("xv")], 0.7)

    def count():
        mms([(T.P0[:, 400:416], T.ones[:], T.n2[:], True, True)], [A_("ones"), A_("n2")], [A_("P0")])
        actv(T.aj[:], T.P0[:, 400:416], ACT.Copy, [A_("P0")], [A_("aj"), A_("ac")], 16, scale=-1.0 / 2048, accum_out=T.ac[:, 0:1])
        tcopy(T.aci[:, 0:1], T.ac[:, 0:1], [A_("ac")], [A_("aci")], 1)
        ts(T.acm[:, 0:1], T.aci[:, 0:1], 31, None, ALU.bitwise_and, None, [A_("aci")], [A_("acm")])
        ts(T.a8[:, 0:1], T.acm[:, 0:1], 8.0, None, ALU.mult, None, [A_("acm")], [A_("a8")])
        ts(T.THe[:], T.TH[:], T.a8[:, 0:1], None, ALU.add, None, [A_("TH"), A_("a8")], [A_("THe")], 128)

    G = [[0, 1, 2, 3], [4, 5, 6, 7], [8, 9, 10, 11], [12, 13, 14, 15], [16]]
    tcopy(T.THe[:], T.TH[:], [A_("TH")], [A_("THe")], 128)
    for t in range(NV):
        rho, W = GSH[t], "W%d" % t
        def part(name, f, *args):
            tag[0] = name + "z" if t == 0 and name + "z" in BOOST else name
            f(*args)
            tag[0] = ""

        for h in range(2):
            s = str(h)
            w, RW = L128(h)
            part("x" + s, values, t, h)
            part("u" + s, u_sum, h)
            part("e" + s, expand, h)
            part("r" + s, relators, t, h)
            part("w" + s, tcopy, T.w16[:, w], T[W][:, w], [RW(W)], [RW("w16")], 64)
            part("t" + s, new_words, h, G[0], rho)
            part("t" + s, new_words, h, G[1], rho)
            part("d" + s, distances, "rl", "X0", h, True)
            if t < NRT:
                part("o" + s, rotations, h)
        part("su", spread_u)
        part("at", at_list)
        for h in range(2):
            s = str(h)
            part("l" + s, least, t, h)
            part("m" + s, misc, 128 * h, 128 * h + 128)
            part("g" + s, distances, "ql", "xw", h, False)
            part("v" + s, new_values, h)
            for j in (2, 3, 4):
                part("n" + s, new_words, h, G[j], rho)
        for h in range(2):
            part("k" + str(h), match, h, rho)
            part("s" + str(h), send, t, h)
        part("wl", write_values)
        if t < NV - 1:
            part("ct", count)

    dma("y", T.yx[:], T.xv[:, 0:V], [A_("xv", 0, V)], [], "out0", 16, 5.0)
    c, rc = cmat(REV, 0)
    mms([(T.E0[:, 0:256], c, T.yf[:], True, True)], rc + [A_("yf")], [A_("E0")], 256)
    tcopy(T.yo[:], T.E0[:, 0:256], [A_("E0")], [A_("yo")])
    dma("s", T.yw[:], T.yo[:], [A_("yo")], [], "out1", 16, 3.0)

    Q = {"v": g.vector, "s": g.scalar, "t": g.tensor, "g": g, "y": g.sync}
    cnt = {q: 0 for q in Q}
    seen = {q: {} for q in Q}
    snap, acc = {}, {}

    def need(q, tok):
        s, val = tok
        if seen[q].get(s, 0) >= val:
            return
        Q[q].wait_ge(T.sem[s], val)
        seen[q][s] = val
        for s2, v2 in snap.get(tok, {}).items():
            if seen[q].get(s2, 0) < v2:
                seen[q][s2] = v2

    def deps(q, reads, writes):
        toks = {}
        for regs, wr in ((reads, False), (writes, True)):
            for b, lo, hi in regs:
                for l2, h2, q2, tok, w2 in acc.get(b, ()):
                    if b in PSUM:
                        if q2 == q:
                            continue
                    elif l2 >= hi or h2 <= lo or not (wr or w2):
                        continue
                    toks[tok[0]] = max(toks.get(tok[0], 0), tok[1])
        for s in sorted(toks):
            need(q, (s, toks[s]))

    def note(q, reads, writes, tok):
        snap[tok] = dict(seen[q if q in seen else "g"]) if q in seen else {}
        for regs, wr in ((reads, False), (writes, True)):
            for b, lo, hi in regs:
                old = acc.get(b, [])
                if b in PSUM:
                    acc[b] = [[lo, hi, q, tok, True]]
                elif wr:
                    acc[b] = [e for e in old if not (e[0] >= lo and e[1] <= hi)] + [[lo, hi, q, tok, True]]
                else:
                    acc[b] = [e for e in old if not (e[2] == q and not e[4] and e[0] >= lo and e[1] <= hi)] + [[lo, hi, q, tok, False]]

    for t in range(1, NV):
        for h in range(2):
            acc.setdefault("W%d" % t, []).append([128 * h, 128 * h + 128, "remote", ("ar%d_%d" % (t, h), n_in), True])
    for i in schedule(ops):
        o = ops[i]
        q = o["q"]
        if o["kind"] == "r":
            deps(q, o["r"], [])
            o["f"][0]()
        elif o["kind"] == "d":
            deps(q, o["r"], o["w"])
            sem, total = o["sem"]
            o["f"][0]().then_inc(T.sem[sem], 16)
            before = dict(seen[q])
            note("dma", o["r"], o["w"], (sem, total))
            snap[(sem, total)] = before
        else:
            deps(q, o["r"], o["w"])
            for f in o["f"]:
                cnt[q] += 1
                f().then_inc(T.sem["q" + q], 1)
            note(q, o["r"], o["w"], ("q" + q, cnt[q]))
    for q in ("v", "s", "t", "g"):
        need("g", ("q" + q, cnt[q]))
    for k in range(6):
        need("g", ("ld%d" % k, 16))
    for t in range(1, NV):
        for h in range(2):
            need("g", ("ar%d_%d" % (t, h), n_in))
    for s, val in (("rd", 32), ("rtl", 256), ("ls", 2 * (NV - 1) * n_out), ("out0", 16), ("out1", 16)):
        need("g", (s, val))
